import numpy as np
import ml_dtypes


def mxq(x, axis, fmt="e4m3"):
    dtype, down = {"e4m3": (ml_dtypes.float8_e4m3fn, 7), "e5m2": (ml_dtypes.float8_e5m2, 14)}[fmt]
    v = np.moveaxis(np.asarray(x, np.float32).astype(ml_dtypes.bfloat16).astype(np.float64), axis, -1)
    blocks = v.reshape(v.shape[:-1] + (-1, 32))
    amax = np.abs(blocks).max(-1, keepdims=True)
    byte = np.maximum(np.where(amax > 0, np.frexp(amax)[1] - 1 + 127, 0) - down, 1)
    scale = np.exp2(byte - 127.0)
    codes = (blocks / scale).astype(np.float32).astype(dtype).astype(np.float64)
    return np.moveaxis((codes * scale).reshape(v.shape), -1, axis)


WIDE = False


def mx_kscale(k):
    if not WIDE:
        return np.ones(k)
    levels = np.array([30, -30])
    if k % 512:
        return np.exp2(np.random.permutation(np.resize(levels, k // 32))).repeat(32)
    a = np.empty((k // 512, 16))
    for p in range(k // 512):
        a[p, :8] = np.random.permutation(np.resize(levels, 8))
        for g in range(8):
            far = levels[np.abs(levels - a[p, g]) >= 10]
            a[p, g + 8] = far[np.random.randint(len(far))]
    return np.exp2(a.ravel()).repeat(32)


BF16 = ml_dtypes.bfloat16


def bf(x):
    return np.asarray(x, np.float32).astype(BF16)


def f64(x):
    return np.asarray(x).astype(np.float64)


E2M1 = np.array([0.0, 0.5, 1.0, 1.5, 2.0, 3.0, 4.0, 6.0, -0.0, -0.5, -1.0, -1.5, -2.0, -3.0, -4.0, -6.0])


def pack_weight(w, fmt):
    k, n = w.shape
    w = f64(bf(w)).reshape(k // 32, 32, n)
    amax = np.abs(w).max(1)
    if fmt == "e4m3":
        byte = np.frexp(amax)[1] - 1 + 127 - 7
    else:
        mant, ex = np.frexp(amax / 6.0)
        byte = np.where(mant > 0.5, ex, ex - 1) + 127
    byte = np.clip(np.where(amax > 0, byte, 1), 1, 254)
    scaled = (w * np.exp2(127.0 - byte)[:, None, :]).reshape(k, n).astype(np.float32)
    by_word = np.ascontiguousarray(scaled.reshape(k // 512, 128, 4, n).transpose(0, 1, 3, 2))
    if fmt == "e4m3":
        words = by_word.astype(ml_dtypes.float8_e4m3fn).view(np.uint8)
    else:
        c = by_word.astype(ml_dtypes.float4_e2m1fn).view(np.uint8) & 0xF
        words = c[..., 0::2] | (c[..., 1::2] << 4)
    return np.ascontiguousarray(words), np.ascontiguousarray(byte.astype(np.uint8).reshape(k // 512, 16, n))


def unpack_weight(words, scales, fmt):
    g, p, n, _ = words.shape
    if fmt == "e4m3":
        vals = np.ascontiguousarray(words).view(ml_dtypes.float8_e4m3fn).astype(np.float64)
    else:
        nib = np.empty((g, p, n, 4), np.uint8)
        nib[..., 0::2] = words & 0xF
        nib[..., 1::2] = words >> 4
        vals = E2M1[nib]
    vals = vals * np.repeat(np.exp2(scales.astype(np.float64) - 127.0), 8, axis=1)[..., None]
    return vals.transpose(0, 1, 3, 2).reshape(g * 512, n)
def pack4(w):
    words, scales = pack_weight(w, "e2m1")
    return words.reshape(words.shape[0], 128, -1), scales


def unpack4(words, scales):
    return unpack_weight(words.reshape(words.shape[0], 128, -1, 2), scales, "e2m1")


D, C, A, F = 1024, 1024, 2048, 1024
B_STD = 0.3
CORR_STD = 0.1


def setup_inputs():
    s = mx_kscale(C)
    t = mx_kscale(A)
    w = np.random.standard_normal((C, A)) / np.sqrt(C) / s[:, None]
    w_words, w_scales = pack4(w)
    return {"x": bf(np.random.standard_normal((D, C)) * s),
            "w_words": w_words,
            "w_scales": w_scales,
            "b": bf(B_STD * np.random.standard_normal(A)),
            "corr": bf((1 + CORR_STD * np.random.standard_normal(A)) * t),
            "rain": bf(np.random.standard_normal((A, F)) / np.sqrt(A) / t[:, None])}


def reference(x, w_words, w_scales, b, corr, rain):
    w = unpack4(w_words, w_scales)
    score = mxq(f64(x), 1, "e4m3") @ w
    kern = np.exp(score + f64(b))
    mean = kern.mean(axis=1, keepdims=True)
    h = kern * f64(corr)
    y = mxq(h, 1, "e5m2") @ mxq(f64(rain), 0, "e4m3")
    return y / mean

@@ -1,0 +1,380 @@
+from contextlib import ExitStack
+
+import concourse.mybir as mybir
+from concourse.masks import make_identity
+
+D, C, A, F = 1024, 1024, 2048, 1024
+FLOPS = 2 * D * C * A + 2 * D * A * F
+
+F32 = mybir.dt.float32
+BF16 = mybir.dt.bfloat16
+I32 = mybir.dt.int32
+U32 = mybir.dt.uint32
+U8 = mybir.dt.uint8
+E4M3 = mybir.dt.float8_e4m3fn_x4
+E5M2 = mybir.dt.float8_e5m2_x4
+E2M1 = mybir.dt.float4_e2m1fn_x4
+ACT = mybir.ActivationFunctionType
+ALU = mybir.AluOpType
+
+P = 128
+N = 512
+WARM = 4
+
+
+def tile_analogue_rain_downscaling_s9_kernel(tc, x, w_words, w_scales, b, corr, rain, out):
+    nc = tc.nc
+    with ExitStack() as ctx:
+        keep = ctx.enter_context(tc.tile_pool(name="keep", bufs=1))
+        psum = ctx.enter_context(tc.psum_pool(name="psum", bufs=1))
+        ctx.enter_context(tc.manual_schedule())
+
+        def bank(i, shape, name):
+            return psum.tile(shape, F32, name=name, tag="bank%d" % i)
+
+        s_raw = keep.tile([P, 2, A // 4], I32, name="s_raw", align_bytes=64)
+        bc_rows = keep.tile([P, N], BF16, name="bc_rows", align_bytes=64)
+        zeros = keep.tile([P, N], BF16, name="zeros", align_bytes=64)
+        ident = keep.tile([P, P], F32, name="ident", align_bytes=64)
+        nc.vector.memset(bc_rows[:], 0.0)
+        make_identity(nc, ident[:])
+        nc.vector.memset(zeros[:], 0.0)
+        nc.vector.memset(s_raw[:], 0)
+        table = keep.tile([P, 1], F32, name="table")
+        nc.scalar.activation(out=table[:], in_=zeros[:, 0:1], func=ACT.Exp)
+
+        x_raw, w_raw, r_raw = {}, {}, {}
+
+        def load_x(hf, k):
+            x_raw[hf, k] = keep.tile([P, 4, N], BF16, name="x_raw%d%d" % (hf, k), align_bytes=64)
+            src = x[N * hf : N * (hf + 1), N * k : N * (k + 1)].rearrange("(j p) c -> p j c", p=P)
+            nc.sync.dma_start(out=x_raw[hf, k][:], in_=src)
+
+        def load_w(g):
+            w_raw[g] = keep.tile([P, 2, 256], I32, name="w_raw%d" % g, align_bytes=64)
+            src = w_words.bitcast(I32).rearrange("k p n -> p k n")[:, :, 256 * g : 256 * (g + 1)]
+            nc.sync.dma_start(out=w_raw[g][:], in_=src)
+
+        def load_scales():
+            src = w_scales.bitcast(I32).rearrange("k q n -> q k n")
+            for q in range(4):
+                nc.sync.dma_start(out=s_raw[32 * q : 32 * q + 4, :, :], in_=src[4 * q : 4 * q + 4, :, :])
+
+        def load_rain(g):
+            r_raw[g] = keep.tile([P, 4, F], BF16, name="r_raw%d" % g, align_bytes=64)
+            src = rain[N * g : N * (g + 1), :].rearrange("(m t e) f -> e m t f", t=4, e=4)
+            for e in range(4):
+                nc.sync.dma_start(out=r_raw[g][e:P:4, :, :], in_=src[e])
+
+        load_x(0, 0)
+        load_x(0, 1)
+        nc.gpsimd.dma_start(out=bc_rows[0:4, :], in_=b.rearrange("(g a) -> g a", g=4))
+        nc.gpsimd.dma_start(out=bc_rows[4:8, :], in_=corr.rearrange("(g a) -> g a", g=4))
+        load_scales()
+        load_w(0)
+        load_w(1)
+        load_rain(0)
+        load_x(1, 0)
+        load_x(1, 1)
+        load_w(2)
+        load_w(3)
+        load_rain(1)
+        load_rain(2)
+        load_rain(3)
+
+        def warm(n):
+            scratch = bank(0, [P, N], "scratch")
+            for i in range(n):
+                nc.tensor.matmul(out=scratch[:], lhsT=zeros[:, 0:P], rhs=zeros[:], start=True, stop=True)
+
+        x_ps, x_il, x_q, x_s = {}, {}, {}, {}
+
+        def x_turn(hf, k, jj, bk):
+            ps = bank(bk, [P, 2, 2, P], "x_ps%d%d%d" % (hf, k, jj))
+            x_ps[hf, k, jj] = ps
+            for j in range(2):
+                words = x_raw[hf, k][:, 2 * jj + j, :].bitcast(F32)
+                for u in range(2):
+                    nc.tensor.transpose(ps[:, j, u, :], words[:, u:256:2], ident[:])
+
+        def x_out(hf, k, jj, on_vector):
+            if (hf, k) not in x_il:
+                x_il[hf, k] = keep.tile([P, 4 * N], BF16, name="x_il%d%d" % (hf, k), tag="x_il", bufs=2, align_bytes=64)
+            dst = x_il[hf, k][:, 1024 * jj : 1024 * (jj + 1)].bitcast(F32).rearrange("p (j r u) -> p j r u", j=2, u=2)
+            src = x_ps[hf, k, jj][:].rearrange("p j u r -> p j r u")
+            if on_vector:
+                nc.vector.tensor_copy(out=dst, in_=src)
+            else:
+                nc.scalar.copy(out=dst, in_=src)
+
+        def x_quant(hf, k):
+            x_q[hf, k] = keep.tile([P, N], U32, name="x_q%d%d" % (hf, k), align_bytes=64)
+            x_s[hf, k] = keep.tile([P, N], U8, name="x_s%d%d" % (hf, k), align_bytes=64)
+            nc.vector.quantize_mx(out=x_q[hf, k][:].bitcast(E4M3), scales=x_s[hf, k][:], in_=x_il[hf, k][:])
+
+        w_q, w_s = {}, {}
+
+        def w_sort(g):
+            w_q[g] = keep.tile([P, 2 * 1024], U8, name="w_q%d" % g, align_bytes=64)
+            nc.vector.tensor_copy(
+                out=w_q[g][:].bitcast(I32).rearrange("p (k t m i) -> p k t m i", k=2, t=4, i=2),
+                in_=w_raw[g][:].rearrange("p k (m t i) -> p k t m i", t=4, i=2),
+            )
+
+        def s_sort(g):
+            w_s[g] = keep.tile([P, 2 * N], U8, name="w_s%d" % g, align_bytes=64)
+            nc.vector.tensor_copy(
+                out=w_s[g][:].bitcast(I32).rearrange("p (k t m) -> p k t m", k=2, t=4),
+                in_=s_raw[:, :, P * g : P * (g + 1)].rearrange("p k (m t) -> p k t m", t=4),
+            )
+
+        bc_sorted = keep.tile([P, 4, P], F32, name="bc_sorted", align_bytes=64)
+        bias = keep.tile([P, 4, 4], F32, name="bias", align_bytes=64)
+        gain = keep.tile([P, 4, 4, 2], F32, name="gain", align_bytes=64)
+
+        def bc_sort():
+            nc.vector.tensor_copy(
+                out=bc_sorted[:].rearrange("p t (m e) -> p t m e", e=4),
+                in_=bc_rows[:].rearrange("p (m t e) -> p t m e", t=4, e=4),
+            )
+
+        bc_ps = {}
+
+        def bc_turn_pe(bk):
+            bc_ps[0] = bank(bk, [P, 4, P], "bc_ps")
+            for t in range(4):
+                nc.tensor.transpose(bc_ps[0][:, t, :], bc_sorted[:, t, :], ident[:])
+
+        def bc_out():
+            ps = bc_ps[0]
+            nc.scalar.copy(out=bias[:], in_=ps[:, :, 0:4].rearrange("p t g -> p g t"))
+            nc.scalar.copy(out=gain[:], in_=ps[:, :, 4:8].rearrange("p t g -> p g t").unsqueeze(3).to_broadcast([P, 4, 4, 2]))
+
+        r_il, r_q, r_s = {}, {}, {}
+
+        def r_weave(g, fh, part, on_vector):
+            if (g, fh) not in r_il:
+                r_il[g, fh] = keep.tile([P, 4 * N], BF16, name="r_il%d%d" % (g, fh), tag="r_il", bufs=3, align_bytes=64)
+            lo, hi = ((0, 256), (256, N), (0, N))[part]
+            dst = r_il[g, fh][:, 4 * lo : 4 * hi].rearrange("p (c i t) -> p c t i", i=4, t=4)
+            src = r_raw[g][:, :, N * fh + lo : N * fh + hi].rearrange("p t (c i) -> p c t i", i=4)
+            if on_vector:
+                nc.vector.tensor_copy(out=dst, in_=src)
+            else:
+                nc.scalar.copy(out=dst, in_=src)
+
+        def r_quant(g, fh):
+            r_q[g, fh] = keep.tile([P, N], U32, name="r_q%d%d" % (g, fh), align_bytes=64)
+            r_s[g, fh] = keep.tile([P, N], U8, name="r_s%d%d" % (g, fh), align_bytes=64)
+            nc.vector.quantize_mx(out=r_q[g, fh][:].bitcast(E4M3), scales=r_s[g, fh][:], in_=r_il[g, fh][:])
+
+        kern, h_il, h_q, h_s = {}, {}, {}, {}
+
+        def score(hf, g, t, bk):
+            if t == 0:
+                kern[hf, g] = keep.tile([P, 4, N], F32, name="kern%d%d" % (hf, g), tag="kern", bufs=5, align_bytes=64)
+            ps = bank(bk, [P, N], "sc%d%d%d" % (hf, g, t))
+            for k in range(2):
+                c0 = 1024 * k + 256 * t
+                s0 = N * k + P * t
+                nc.tensor.matmul_mx(
+                    out=ps[:],
+                    lhsT=w_q[g][:, c0 : c0 + 256].bitcast(E2M1),
+                    lhsT_scale=w_s[g][:, s0 : s0 + P],
+                    rhs=x_q[hf, k][:].bitcast(E4M3),
+                    rhs_scale=x_s[hf, k][:],
+                    start=(k == 0),
+                    stop=(k == 1),
+                )
+            nc.scalar.activation(out=kern[hf, g][:, t, :], in_=ps[:], func=ACT.Exp, bias=bias[:, g, t : t + 1])
+
+        def h_make(hf, g):
+            h_il[hf, g] = keep.tile([P, 4 * N], BF16, name="h_il%d%d" % (hf, g), tag="h_il", bufs=2, align_bytes=64)
+            nc.vector.tensor_tensor(
+                out=h_il[hf, g][:].rearrange("p (c i t) -> p c t i", i=2, t=4),
+                in0=kern[hf, g][:].rearrange("p t (c i) -> p c t i", i=2),
+                in1=gain[:, g, :, :].unsqueeze(1).to_broadcast([P, N // 2, 4, 2]),
+                op=ALU.mult,
+            )
+
+        def h_quant(hf, g):
+            h_q[hf, g] = keep.tile([P, N], U32, name="h_q%d%d" % (hf, g), align_bytes=64)
+            h_s[hf, g] = keep.tile([P, N], U8, name="h_s%d%d" % (hf, g), align_bytes=64)
+            nc.vector.quantize_mx(out=h_q[hf, g][:].bitcast(E5M2), scales=h_s[hf, g][:], in_=h_il[hf, g][:])
+
+        m_ps, inv = {}, {}
+
+        def mean_add(hf, rows, bk, first, last):
+            if first:
+                m_ps[hf] = bank(bk, [P, 4, P], "m_ps%d" % hf)
+            for i, row in enumerate(rows):
+                for j in range(4):
+                    nc.tensor.matmul(
+                        out=m_ps[hf][:, j, :],
+                        lhsT=row[:, P * j : P * (j + 1)],
+                        rhs=ident[:],
+                        is_transpose=True,
+                        start=(first and i == 0 and j == 0),
+                        stop=(last and i == len(rows) - 1 and j == 3),
+                    )
+
+        def kern_rows(hf, g):
+            return [kern[hf, g][:, t, :] for t in range(4)]
+
+        def add(name, a, c):
+            res = keep.tile(list(a.shape), F32, name=name, align_bytes=64)
+            nc.vector.tensor_tensor(out=res[:], in0=a, in1=c, op=ALU.add)
+            return res
+
+        def mean_end(hf):
+            total = keep.tile([P, 4], F32, name="total%d" % hf)
+            mean = keep.tile([P, 4], F32, name="mean%d" % hf)
+            inv[hf] = keep.tile([P, 4], F32, name="inv%d" % hf)
+            nc.vector.tensor_reduce(out=total[:], in_=m_ps[hf][:], axis=mybir.AxisListType.X, op=ALU.add)
+            nc.vector.tensor_scalar(out=mean[:], in0=total[:], scalar1=1.0 / A, scalar2=None, op0=ALU.mult)
+            nc.vector.reciprocal(out=inv[hf][:], in_=mean[:])
+
+        y_ps = {}
+
+        def y_pass(hf, j, fh, g, bk):
+            if g == 0:
+                y_ps[hf, j, fh] = bank(bk, [P, N], "y%d%d%d" % (hf, j, fh))
+            nc.tensor.matmul_mx(
+                out=y_ps[hf, j, fh][:],
+                lhsT=h_q[hf, g][:, P * j : P * (j + 1)].bitcast(E5M2),
+                lhsT_scale=h_s[hf, g][:, P * j : P * (j + 1)],
+                rhs=r_q[g, fh][:].bitcast(E4M3),
+                rhs_scale=r_s[g, fh][:],
+                start=(g == 0),
+                stop=(g == 3),
+            )
+
+        def y_out(hf, j, fh, on_vector):
+            res = keep.tile([P, N], F32, name="res%d%d%d" % (hf, j, fh), tag="res", bufs=6, align_bytes=64)
+            if on_vector:
+                nc.vector.tensor_scalar(out=res[:], in0=y_ps[hf, j, fh][:], scalar1=inv[hf][:, j : j + 1], scalar2=None, op0=ALU.mult)
+            else:
+                nc.scalar.activation(out=res[:], in_=y_ps[hf, j, fh][:], func=ACT.Copy, scale=inv[hf][:, j : j + 1])
+            r0 = N * hf + P * j
+            nc.sync.dma_start(out=out[r0 : r0 + P, N * fh : N * (fh + 1)], in_=res[:])
+
+        def y_group(hf, j, fh, bk, on_vector):
+            for g in range(4):
+                y_pass(hf, j, fh, g, bk)
+            y_out(hf, j, fh, on_vector)
+
+        def scores(hf, g):
+            for t in range(4):
+                score(hf, g, t, t)
+
+        V, S = True, False
+        warm(WARM)
+        x_turn(0, 0, 0, 4)
+        x_turn(0, 0, 1, 5)
+        warm(2)
+        x_out(0, 0, 0, S)
+        x_out(0, 0, 1, S)
+        x_turn(0, 1, 0, 6)
+        x_turn(0, 1, 1, 7)
+        bc_sort()
+        bc_turn_pe(3)
+        warm(3)
+        x_quant(0, 0)
+        x_out(0, 1, 0, S)
+        x_out(0, 1, 1, V)
+        bc_out()
+        s_sort(0)
+        w_sort(0)
+        x_quant(0, 1)
+        s_sort(1)
+        w_sort(1)
+
+        scores(0, 0)
+        r_weave(0, 0, 2, V)
+        s_sort(2)
+        w_sort(2)
+        r_quant(0, 0)
+        h_make(0, 0)
+
+        score(0, 1, 0, 0)
+        score(0, 1, 1, 1)
+        x_turn(1, 0, 0, 5)
+        x_turn(1, 0, 1, 6)
+        score(0, 1, 2, 2)
+        score(0, 1, 3, 3)
+        mean_add(0, kern_rows(0, 0), 4, True, False)
+        x_out(1, 0, 0, S)
+        x_out(1, 0, 1, S)
+        r_weave(0, 1, 2, V)
+        h_quant(0, 0)
+        s_sort(3)
+        w_sort(3)
+        h_make(0, 1)
+
+        score(0, 2, 0, 0)
+        score(0, 2, 1, 1)
+        x_turn(1, 1, 0, 7)
+        x_turn(1, 1, 1, 5)
+        score(0, 2, 2, 2)
+        score(0, 2, 3, 3)
+        mean_add(0, kern_rows(0, 1), 4, False, False)
+        x_out(1, 1, 0, S)
+        x_out(1, 1, 1, S)
+        r_quant(0, 1)
+        h_quant(0, 1)
+        r_weave(1, 0, 2, V)
+        x_quant(1, 0)
+        h_make(0, 2)
+
+        scores(0, 3)
+        mean_add(0, kern_rows(0, 2), 4, False, False)
+        r_weave(2, 0, 0, S)
+        x_quant(1, 1)
+        h_quant(0, 2)
+        r_quant(1, 0)
+        h_make(0, 3)
+
+        scores(1, 0)
+        mean_add(0, kern_rows(0, 3), 4, False, True)
+        r_weave(2, 0, 1, S)
+        r_weave(3, 0, 0, V)
+        h_quant(0, 3)
+        mean_end(0)
+        h_make(1, 0)
+
+        scores(1, 1)
+        mean_add(1, kern_rows(1, 0), 4, True, False)
+        r_weave(3, 0, 1, S)
+        r_quant(2, 0)
+        h_quant(1, 0)
+        h_make(1, 1)
+
+        scores(1, 2)
+        mean_add(1, kern_rows(1, 1), 4, False, False)
+        r_weave(1, 1, 0, S)
+        r_quant(3, 0)
+        h_quant(1, 1)
+        r_weave(1, 1, 1, V)
+        h_make(1, 2)
+
+        scores(1, 3)
+        r_weave(2, 1, 2, S)
+        r_quant(1, 1)
+        r_weave(3, 1, 2, V)
+        h_quant(1, 2)
+        r_quant(3, 1)
+        r_quant(2, 1)
+        for j in range(4):
+            y_group(0, j, 0, (5, 6, 7, 0)[j], S)
+        pa = add("pa", kern[1, 2][:, 0:2, :], kern[1, 2][:, 2:4, :])
+        pb = add("pb", kern[1, 3][:, 0:2, :], kern[1, 3][:, 2:4, :])
+        h_make(1, 3)
+        for j in range(3):
+            y_group(0, j, 1, (1, 2, 3)[j], S)
+        mean_add(1, [pa[:, 0, :], pa[:, 1, :], pb[:, 0, :], pb[:, 1, :]], 4, False, True)
+        y_group(0, 3, 1, 5, S)
+        h_quant(1, 3)
+        mean_end(1)
+        for j in range(4):
+            for fh in range(2):
+                y_group(1, j, fh, (6, 7, 0, 1, 2, 3, 5, 6)[2 * j + fh], fh == 1)

@@ -32,14 +32,15 @@ def tile_analogue_rain_downscaling_s9_kernel(tc, x, w_words, w_scales, b, corr, 
         def bank(i, shape, name):
             return psum.tile(shape, F32, name=name, tag="bank%d" % i)
 
-        s_raw = keep.tile([P, 2, A // 4], I32, name="s_raw", align_bytes=64)
+        s_raw = [keep.tile([P, 2, P], I32, name="s_raw0", align_bytes=64), keep.tile([P, 2, 3 * P], I32, name="s_raw1", align_bytes=64)]
         bc_rows = keep.tile([P, N], BF16, name="bc_rows", align_bytes=64)
         zeros = keep.tile([P, N], BF16, name="zeros", align_bytes=64)
         ident = keep.tile([P, P], F32, name="ident", align_bytes=64)
-        nc.vector.memset(bc_rows[:], 0.0)
-        make_identity(nc, ident[:])
         nc.vector.memset(zeros[:], 0.0)
-        nc.vector.memset(s_raw[:], 0)
+        nc.vector.memset(bc_rows[:], 0.0)
+        nc.vector.memset(s_raw[0][:], 0)
+        nc.vector.memset(s_raw[1][:], 0)
+        make_identity(nc, ident[:])
         table = keep.tile([P, 1], F32, name="table")
         nc.scalar.activation(out=table[:], in_=zeros[:, 0:1], func=ACT.Exp)
 
@@ -50,15 +51,18 @@ def tile_analogue_rain_downscaling_s9_kernel(tc, x, w_words, w_scales, b, corr, 
             src = x[N * hf : N * (hf + 1), N * k : N * (k + 1)].rearrange("(j p) c -> p j c", p=P)
             nc.sync.dma_start(out=x_raw[hf, k][:], in_=src)
 
-        def load_w(g):
-            w_raw[g] = keep.tile([P, 2, 256], I32, name="w_raw%d" % g, align_bytes=64)
-            src = w_words.bitcast(I32).rearrange("k p n -> p k n")[:, :, 256 * g : 256 * (g + 1)]
-            nc.sync.dma_start(out=w_raw[g][:], in_=src)
+        def load_w(g0, g1):
+            raw = keep.tile([P, 2, 256 * (g1 - g0)], I32, name="w_raw%d" % g0, align_bytes=64)
+            src = w_words.bitcast(I32).rearrange("k p n -> p k n")[:, :, 256 * g0 : 256 * g1]
+            nc.sync.dma_start(out=raw[:], in_=src)
+            for g in range(g0, g1):
+                w_raw[g] = raw[:, :, 256 * (g - g0) : 256 * (g - g0 + 1)]
 
-        def load_scales():
+        def load_scales(i):
+            lo, hi = ((0, P), (P, 4 * P))[i]
             src = w_scales.bitcast(I32).rearrange("k q n -> q k n")
             for q in range(4):
-                nc.sync.dma_start(out=s_raw[32 * q : 32 * q + 4, :, :], in_=src[4 * q : 4 * q + 4, :, :])
+                nc.sync.dma_start(out=s_raw[i][32 * q : 32 * q + 4, :, :], in_=src[4 * q : 4 * q + 4, :, lo:hi])
 
         def load_rain(g):
             r_raw[g] = keep.tile([P, 4, F], BF16, name="r_raw%d" % g, align_bytes=64)
@@ -68,16 +72,16 @@ def tile_analogue_rain_downscaling_s9_kernel(tc, x, w_words, w_scales, b, corr, 
 
         load_x(0, 0)
         load_x(0, 1)
-        nc.gpsimd.dma_start(out=bc_rows[0:4, :], in_=b.rearrange("(g a) -> g a", g=4))
-        nc.gpsimd.dma_start(out=bc_rows[4:8, :], in_=corr.rearrange("(g a) -> g a", g=4))
-        load_scales()
-        load_w(0)
-        load_w(1)
+        nc.sync.dma_start(out=bc_rows[0:4, :], in_=b.rearrange("(g a) -> g a", g=4))
+        nc.sync.dma_start(out=bc_rows[4:8, :], in_=corr.rearrange("(g a) -> g a", g=4))
+        load_w(0, 1)
+        load_scales(0)
+        load_scales(1)
+        load_w(1, 2)
         load_rain(0)
+        load_w(2, 4)
         load_x(1, 0)
         load_x(1, 1)
-        load_w(2)
-        load_w(3)
         load_rain(1)
         load_rain(2)
         load_rain(3)
@@ -118,22 +122,21 @@ def tile_analogue_rain_downscaling_s9_kernel(tc, x, w_words, w_scales, b, corr, 
             w_q[g] = keep.tile([P, 2 * 1024], U8, name="w_q%d" % g, align_bytes=64)
             nc.vector.tensor_copy(
                 out=w_q[g][:].bitcast(I32).rearrange("p (k t m i) -> p k t m i", k=2, t=4, i=2),
-                in_=w_raw[g][:].rearrange("p k (m t i) -> p k t m i", t=4, i=2),
+                in_=w_raw[g].rearrange("p k (m t i) -> p k t m i", t=4, i=2),
             )
 
         def s_sort(g):
             w_s[g] = keep.tile([P, 2 * N], U8, name="w_s%d" % g, align_bytes=64)
             nc.vector.tensor_copy(
                 out=w_s[g][:].bitcast(I32).rearrange("p (k t m) -> p k t m", k=2, t=4),
-                in_=s_raw[:, :, P * g : P * (g + 1)].rearrange("p k (m t) -> p k t m", t=4),
+                in_=(s_raw[0][:] if g == 0 else s_raw[1][:, :, P * (g - 1) : P * g]).rearrange("p k (m t) -> p k t m", t=4),
             )
 
         bc_sorted = keep.tile([P, 4, P], F32, name="bc_sorted", align_bytes=64)
         bias = keep.tile([P, 4, 4], F32, name="bias", align_bytes=64)
-        gain = keep.tile([P, 4, 4, 2], F32, name="gain", align_bytes=64)
 
         def bc_sort():
-            nc.vector.tensor_copy(
+            nc.scalar.copy(
                 out=bc_sorted[:].rearrange("p t (m e) -> p t m e", e=4),
                 in_=bc_rows[:].rearrange("p (m t e) -> p t m e", t=4, e=4),
             )
@@ -148,13 +151,12 @@ def tile_analogue_rain_downscaling_s9_kernel(tc, x, w_words, w_scales, b, corr, 
         def bc_out():
             ps = bc_ps[0]
             nc.scalar.copy(out=bias[:], in_=ps[:, :, 0:4].rearrange("p t g -> p g t"))
-            nc.scalar.copy(out=gain[:], in_=ps[:, :, 4:8].rearrange("p t g -> p g t").unsqueeze(3).to_broadcast([P, 4, 4, 2]))
 
         r_il, r_q, r_s = {}, {}, {}
 
         def r_weave(g, fh, part, on_vector):
             if (g, fh) not in r_il:
-                r_il[g, fh] = keep.tile([P, 4 * N], BF16, name="r_il%d%d" % (g, fh), tag="r_il", bufs=3, align_bytes=64)
+                r_il[g, fh] = keep.tile([P, 4 * N], BF16, name="r_il%d%d" % (g, fh), tag="r_il", bufs=5, align_bytes=64)
             lo, hi = ((0, 256), (256, N), (0, N))[part]
             dst = r_il[g, fh][:, 4 * lo : 4 * hi].rearrange("p (c i t) -> p c t i", i=4, t=4)
             src = r_raw[g][:, :, N * fh + lo : N * fh + hi].rearrange("p t (c i) -> p c t i", i=4)
@@ -189,11 +191,11 @@ def tile_analogue_rain_downscaling_s9_kernel(tc, x, w_words, w_scales, b, corr, 
             nc.scalar.activation(out=kern[hf, g][:, t, :], in_=ps[:], func=ACT.Exp, bias=bias[:, g, t : t + 1])
 
         def h_make(hf, g):
-            h_il[hf, g] = keep.tile([P, 4 * N], BF16, name="h_il%d%d" % (hf, g), tag="h_il", bufs=2, align_bytes=64)
+            h_il[hf, g] = keep.tile([P, 4 * N], BF16, name="h_il%d%d" % (hf, g), tag="h_il%d" % g, align_bytes=64)
             nc.vector.tensor_tensor(
                 out=h_il[hf, g][:].rearrange("p (c i t) -> p c t i", i=2, t=4),
                 in0=kern[hf, g][:].rearrange("p t (c i) -> p c t i", i=2),
-                in1=gain[:, g, :, :].unsqueeze(1).to_broadcast([P, N // 2, 4, 2]),
+                in1=bc_ps[0][:, :, 4 + g : 5 + g].unsqueeze(1).to_broadcast([P, N // 2, 4, 2]),
                 op=ALU.mult,
             )
 
@@ -218,6 +220,29 @@ def tile_analogue_rain_downscaling_s9_kernel(tc, x, w_words, w_scales, b, corr, 
                         stop=(last and i == len(rows) - 1 and j == 3),
                     )
 
+        pair = {}
+
+        def pair_add(hf, g):
+            pair[hf, g] = keep.tile([P, 2, 3 * P], F32, name="pair%d%d" % (hf, g), tag="h_il%d" % ((g - 1) % 4), align_bytes=64)
+            nc.gpsimd.tensor_tensor(out=pair[hf, g][:], in0=kern[hf, g][:, 0:2, 0 : 3 * P], in1=kern[hf, g][:, 2:4, 0 : 3 * P], op=ALU.add)
+
+        def mean_turn(hf, blocks, bk, first, last):
+            if first:
+                m_ps[hf] = bank(bk, [P, 4, P], "m_ps%d" % hf)
+            for i, (j, block) in enumerate(blocks):
+                nc.tensor.matmul(
+                    out=m_ps[hf][:, j, :],
+                    lhsT=block,
+                    rhs=ident[:],
+                    is_transpose=True,
+                    start=(first and i == 0),
+                    stop=(last and i == len(blocks) - 1),
+                )
+
+        def step_blocks(hf, g):
+            blocks = [(3, kern[hf, g][:, t, 3 * P :]) for t in range(4)]
+            return blocks + [(j, pair[hf, g][:, u, P * j : P * (j + 1)]) for u in range(2) for j in range(3)]
+
         def kern_rows(hf, g):
             return [kern[hf, g][:, t, :] for t in range(4)]
 
@@ -226,13 +251,19 @@ def tile_analogue_rain_downscaling_s9_kernel(tc, x, w_words, w_scales, b, corr, 
             nc.vector.tensor_tensor(out=res[:], in0=a, in1=c, op=ALU.add)
             return res
 
-        def mean_end(hf):
-            total = keep.tile([P, 4], F32, name="total%d" % hf)
-            mean = keep.tile([P, 4], F32, name="mean%d" % hf)
+        total, mean = {}, {}
+
+        def mean_sum(hf):
+            total[hf] = keep.tile([P, 4], F32, name="total%d" % hf)
+            nc.vector.tensor_reduce(out=total[hf][:], in_=m_ps[hf][:], axis=mybir.AxisListType.X, op=ALU.add)
+
+        def mean_scale(hf):
+            mean[hf] = keep.tile([P, 4], F32, name="mean%d" % hf)
+            nc.vector.tensor_scalar(out=mean[hf][:], in0=total[hf][:], scalar1=1.0 / A, scalar2=None, op0=ALU.mult)
+
+        def mean_invert(hf):
             inv[hf] = keep.tile([P, 4], F32, name="inv%d" % hf)
-            nc.vector.tensor_reduce(out=total[:], in_=m_ps[hf][:], axis=mybir.AxisListType.X, op=ALU.add)
-            nc.vector.tensor_scalar(out=mean[:], in0=total[:], scalar1=1.0 / A, scalar2=None, op0=ALU.mult)
-            nc.vector.reciprocal(out=inv[hf][:], in_=mean[:])
+            nc.vector.reciprocal(out=inv[hf][:], in_=mean[hf][:])
 
         y_ps = {}
 
@@ -249,132 +280,137 @@ def tile_analogue_rain_downscaling_s9_kernel(tc, x, w_words, w_scales, b, corr, 
                 stop=(g == 3),
             )
 
-        def y_out(hf, j, fh, on_vector):
-            res = keep.tile([P, N], F32, name="res%d%d%d" % (hf, j, fh), tag="res", bufs=6, align_bytes=64)
-            if on_vector:
-                nc.vector.tensor_scalar(out=res[:], in0=y_ps[hf, j, fh][:], scalar1=inv[hf][:, j : j + 1], scalar2=None, op0=ALU.mult)
-            else:
-                nc.scalar.activation(out=res[:], in_=y_ps[hf, j, fh][:], func=ACT.Copy, scale=inv[hf][:, j : j + 1])
+        def y_out(hf, j, fh, on_vector, parts=1):
+            res = keep.tile([P, N], F32, name="res%d%d%d" % (hf, j, fh), tag="res", bufs=5, align_bytes=64)
             r0 = N * hf + P * j
-            nc.sync.dma_start(out=out[r0 : r0 + P, N * fh : N * (fh + 1)], in_=res[:])
+            w = N // parts
+            for c in range(0, N, w):
+                src = y_ps[hf, j, fh][:, c : c + w]
+                if on_vector:
+                    nc.vector.tensor_scalar(out=res[:, c : c + w], in0=src, scalar1=inv[hf][:, j : j + 1], scalar2=None, op0=ALU.mult)
+                else:
+                    nc.scalar.activation(out=res[:, c : c + w], in_=src, func=ACT.Copy, scale=inv[hf][:, j : j + 1])
+                nc.sync.dma_start(out=out[r0 : r0 + P, N * fh + c : N * fh + c + w], in_=res[:, c : c + w])
 
-        def y_group(hf, j, fh, bk, on_vector):
+        def y_group(hf, j, fh, bk, on_vector, parts=1):
             for g in range(4):
                 y_pass(hf, j, fh, g, bk)
-            y_out(hf, j, fh, on_vector)
+            y_out(hf, j, fh, on_vector, parts)
 
         def scores(hf, g):
             for t in range(4):
-                score(hf, g, t, t)
+                score(hf, g, t, (0, 1, 2, 7)[t])
 
         V, S = True, False
         warm(WARM)
         x_turn(0, 0, 0, 4)
         x_turn(0, 0, 1, 5)
-        warm(2)
         x_out(0, 0, 0, S)
-        x_out(0, 0, 1, S)
+        x_out(0, 0, 1, V)
         x_turn(0, 1, 0, 6)
         x_turn(0, 1, 1, 7)
         bc_sort()
         bc_turn_pe(3)
         warm(3)
         x_quant(0, 0)
+        s_sort(0)
         x_out(0, 1, 0, S)
         x_out(0, 1, 1, V)
         bc_out()
-        s_sort(0)
         w_sort(0)
         x_quant(0, 1)
-        s_sort(1)
-        w_sort(1)
 
         scores(0, 0)
+        w_sort(1)
+        for g in range(1, 4):
+            s_sort(g)
         r_weave(0, 0, 2, V)
-        s_sort(2)
         w_sort(2)
-        r_quant(0, 0)
+        w_sort(3)
+        pair_add(0, 0)
         h_make(0, 0)
 
-        score(0, 1, 0, 0)
-        score(0, 1, 1, 1)
+        scores(0, 1)
         x_turn(1, 0, 0, 5)
         x_turn(1, 0, 1, 6)
-        score(0, 1, 2, 2)
-        score(0, 1, 3, 3)
-        mean_add(0, kern_rows(0, 0), 4, True, False)
         x_out(1, 0, 0, S)
         x_out(1, 0, 1, S)
         r_weave(0, 1, 2, V)
         h_quant(0, 0)
-        s_sort(3)
-        w_sort(3)
+        pair_add(0, 1)
         h_make(0, 1)
 
-        score(0, 2, 0, 0)
-        score(0, 2, 1, 1)
-        x_turn(1, 1, 0, 7)
-        x_turn(1, 1, 1, 5)
-        score(0, 2, 2, 2)
-        score(0, 2, 3, 3)
-        mean_add(0, kern_rows(0, 1), 4, False, False)
+        scores(0, 2)
+        x_turn(1, 1, 0, 5)
+        x_turn(1, 1, 1, 6)
         x_out(1, 1, 0, S)
         x_out(1, 1, 1, S)
-        r_quant(0, 1)
-        h_quant(0, 1)
-        r_weave(1, 0, 2, V)
         x_quant(1, 0)
+        r_quant(0, 0)
+        x_quant(1, 1)
+        h_quant(0, 1)
+        pair_add(0, 2)
         h_make(0, 2)
 
         scores(0, 3)
-        mean_add(0, kern_rows(0, 2), 4, False, False)
-        r_weave(2, 0, 0, S)
-        x_quant(1, 1)
+        mean_turn(0, step_blocks(0, 0), 4, True, False)
+        r_weave(1, 0, 0, S)
+        r_quant(0, 1)
+        r_weave(2, 0, 2, V)
         h_quant(0, 2)
-        r_quant(1, 0)
+        pair_add(0, 3)
         h_make(0, 3)
 
         scores(1, 0)
-        mean_add(0, kern_rows(0, 3), 4, False, True)
-        r_weave(2, 0, 1, S)
-        r_weave(3, 0, 0, V)
-        h_quant(0, 3)
-        mean_end(0)
-        h_make(1, 0)
+        mean_turn(0, step_blocks(0, 1), 4, False, False)
+        r_weave(1, 0, 1, S)
+        r_quant(2, 0)
+        r_weave(1, 1, 2, V)
+        r_quant(1, 0)
 
         scores(1, 1)
-        mean_add(1, kern_rows(1, 0), 4, True, False)
-        r_weave(3, 0, 1, S)
-        r_quant(2, 0)
-        h_quant(1, 0)
-        h_make(1, 1)
+        mean_turn(0, step_blocks(0, 2), 4, False, False)
+        r_weave(3, 0, 0, S)
+        h_quant(0, 3)
+        pair_add(1, 0)
+        h_make(1, 0)
 
         scores(1, 2)
-        mean_add(1, kern_rows(1, 1), 4, False, False)
-        r_weave(1, 1, 0, S)
+        mean_turn(0, step_blocks(0, 3), 4, False, True)
+        r_weave(3, 0, 1, S)
+        mean_sum(0)
         r_quant(3, 0)
-        h_quant(1, 1)
-        r_weave(1, 1, 1, V)
-        h_make(1, 2)
+        mean_scale(0)
+        r_quant(1, 1)
+        mean_invert(0)
+        r_weave(2, 1, 2, V)
 
         scores(1, 3)
-        r_weave(2, 1, 2, S)
-        r_quant(1, 1)
-        r_weave(3, 1, 2, V)
-        h_quant(1, 2)
-        r_quant(3, 1)
+        r_weave(3, 1, 2, S)
+        h_quant(1, 0)
+        pair_add(1, 1)
+        h_make(1, 1)
         r_quant(2, 1)
+        r_quant(3, 1)
+        h_quant(1, 1)
+        pair_add(1, 2)
+        h_make(1, 2)
         for j in range(4):
-            y_group(0, j, 0, (5, 6, 7, 0)[j], S)
-        pa = add("pa", kern[1, 2][:, 0:2, :], kern[1, 2][:, 2:4, :])
-        pb = add("pb", kern[1, 3][:, 0:2, :], kern[1, 3][:, 2:4, :])
+            y_group(0, j, 0, (5, 6, 0, 1)[j], S)
+        mean_turn(1, step_blocks(1, 0) + step_blocks(1, 1), 4, True, False)
+        h_quant(1, 2)
+        pair_add(1, 3)
         h_make(1, 3)
-        for j in range(3):
-            y_group(0, j, 1, (1, 2, 3)[j], S)
-        mean_add(1, [pa[:, 0, :], pa[:, 1, :], pb[:, 0, :], pb[:, 1, :]], 4, False, True)
-        y_group(0, 3, 1, 5, S)
-        h_quant(1, 3)
-        mean_end(1)
         for j in range(4):
-            for fh in range(2):
-                y_group(1, j, fh, (6, 7, 0, 1, 2, 3, 5, 6)[2 * j + fh], fh == 1)
+            y_group(0, j, 1, (2, 7, 5, 6)[j], S)
+        h_quant(1, 3)
+        for g in range(3):
+            y_pass(1, 0, 0, g, 0)
+        mean_turn(1, step_blocks(1, 2) + step_blocks(1, 3), 4, False, True)
+        mean_sum(1)
+        mean_scale(1)
+        mean_invert(1)
+        y_pass(1, 0, 0, 3, 0)
+        y_out(1, 0, 0, S)
+        for i in range(1, 8):
+            y_group(1, i // 2, i % 2, (0, 1, 2, 7, 5, 6, 3, 4)[i], i % 2 == 1, 2 if i == 7 else 1)

@@ -19,7 +19,9 @@ ALU = mybir.AluOpType
 
 P = 128
 N = 512
-WARM = 4
+WARM = 3
+PAIRED = (3, 3)
+EARLY = 5
 
 
 def tile_analogue_rain_downscaling_s9_kernel(tc, x, w_words, w_scales, b, corr, rain, out):
@@ -36,20 +38,21 @@ def tile_analogue_rain_downscaling_s9_kernel(tc, x, w_words, w_scales, b, corr, 
         bc_rows = keep.tile([P, N], BF16, name="bc_rows", align_bytes=64)
         zeros = keep.tile([P, N], BF16, name="zeros", align_bytes=64)
         ident = keep.tile([P, P], F32, name="ident", align_bytes=64)
-        nc.vector.memset(zeros[:], 0.0)
         nc.vector.memset(bc_rows[:], 0.0)
+        nc.vector.memset(zeros[:], 0.0)
         nc.vector.memset(s_raw[0][:], 0)
         nc.vector.memset(s_raw[1][:], 0)
         make_identity(nc, ident[:])
         table = keep.tile([P, 1], F32, name="table")
-        nc.scalar.activation(out=table[:], in_=zeros[:, 0:1], func=ACT.Exp)
 
         x_raw, w_raw, r_raw = {}, {}, {}
 
-        def load_x(hf, k):
-            x_raw[hf, k] = keep.tile([P, 4, N], BF16, name="x_raw%d%d" % (hf, k), align_bytes=64)
-            src = x[N * hf : N * (hf + 1), N * k : N * (k + 1)].rearrange("(j p) c -> p j c", p=P)
-            nc.sync.dma_start(out=x_raw[hf, k][:], in_=src)
+        def load_x(hf, k, j0, j1):
+            raw = keep.tile([P, j1 - j0, N], BF16, name="x_raw%d%d%d" % (hf, k, j0), align_bytes=64)
+            src = x[N * hf + P * j0 : N * hf + P * j1, N * k : N * (k + 1)].rearrange("(j p) c -> p j c", p=P)
+            nc.sync.dma_start(out=raw[:], in_=src)
+            for j in range(j0, j1):
+                x_raw[hf, k, j] = raw[:, j - j0, :]
 
         def load_w(g0, g1):
             raw = keep.tile([P, 2, 256 * (g1 - g0)], I32, name="w_raw%d" % g0, align_bytes=64)
@@ -70,18 +73,20 @@ def tile_analogue_rain_downscaling_s9_kernel(tc, x, w_words, w_scales, b, corr, 
             for e in range(4):
                 nc.sync.dma_start(out=r_raw[g][e:P:4, :, :], in_=src[e])
 
-        load_x(0, 0)
-        load_x(0, 1)
-        nc.sync.dma_start(out=bc_rows[0:4, :], in_=b.rearrange("(g a) -> g a", g=4))
-        nc.sync.dma_start(out=bc_rows[4:8, :], in_=corr.rearrange("(g a) -> g a", g=4))
+        nc.scalar.dma_start(out=bc_rows[0:4, :], in_=b.rearrange("(g a) -> g a", g=4))
+        nc.scalar.dma_start(out=bc_rows[4:8, :], in_=corr.rearrange("(g a) -> g a", g=4))
+        nc.scalar.activation(out=table[:], in_=zeros[:, 0:1], func=ACT.Exp)
+        for k in range(2):
+            load_x(0, k, 0, 2)
+            load_x(0, k, 2, 4)
         load_w(0, 1)
         load_scales(0)
-        load_scales(1)
+        load_x(1, 0, 0, 4)
         load_w(1, 2)
-        load_rain(0)
+        load_scales(1)
         load_w(2, 4)
-        load_x(1, 0)
-        load_x(1, 1)
+        load_rain(0)
+        load_x(1, 1, 0, 4)
         load_rain(1)
         load_rain(2)
         load_rain(3)
@@ -97,13 +102,13 @@ def tile_analogue_rain_downscaling_s9_kernel(tc, x, w_words, w_scales, b, corr, 
             ps = bank(bk, [P, 2, 2, P], "x_ps%d%d%d" % (hf, k, jj))
             x_ps[hf, k, jj] = ps
             for j in range(2):
-                words = x_raw[hf, k][:, 2 * jj + j, :].bitcast(F32)
+                words = x_raw[hf, k, 2 * jj + j].bitcast(F32)
                 for u in range(2):
                     nc.tensor.transpose(ps[:, j, u, :], words[:, u:256:2], ident[:])
 
         def x_out(hf, k, jj, on_vector):
             if (hf, k) not in x_il:
-                x_il[hf, k] = keep.tile([P, 4 * N], BF16, name="x_il%d%d" % (hf, k), tag="x_il", bufs=2, align_bytes=64)
+                x_il[hf, k] = keep.tile([P, 4 * N], BF16, name="x_il%d%d" % (hf, k), tag="x_il", bufs=3, align_bytes=64)
             dst = x_il[hf, k][:, 1024 * jj : 1024 * (jj + 1)].bitcast(F32).rearrange("p (j r u) -> p j r u", j=2, u=2)
             src = x_ps[hf, k, jj][:].rearrange("p j u r -> p j r u")
             if on_vector:
@@ -111,10 +116,11 @@ def tile_analogue_rain_downscaling_s9_kernel(tc, x, w_words, w_scales, b, corr, 
             else:
                 nc.scalar.copy(out=dst, in_=src)
 
-        def x_quant(hf, k):
-            x_q[hf, k] = keep.tile([P, N], U32, name="x_q%d%d" % (hf, k), align_bytes=64)
-            x_s[hf, k] = keep.tile([P, N], U8, name="x_s%d%d" % (hf, k), align_bytes=64)
-            nc.vector.quantize_mx(out=x_q[hf, k][:].bitcast(E4M3), scales=x_s[hf, k][:], in_=x_il[hf, k][:])
+        def x_quant(hf, k, c0=0, c1=N):
+            if c0 == 0:
+                x_q[hf, k] = keep.tile([P, N], U32, name="x_q%d%d" % (hf, k), align_bytes=64)
+                x_s[hf, k] = keep.tile([P, N], U8, name="x_s%d%d" % (hf, k), align_bytes=64)
+            nc.vector.quantize_mx(out=x_q[hf, k][:, c0:c1].bitcast(E4M3), scales=x_s[hf, k][:, c0:c1], in_=x_il[hf, k][:, 4 * c0 : 4 * c1])
 
         w_q, w_s = {}, {}
 
@@ -136,7 +142,7 @@ def tile_analogue_rain_downscaling_s9_kernel(tc, x, w_words, w_scales, b, corr, 
         bias = keep.tile([P, 4, 4], F32, name="bias", align_bytes=64)
 
         def bc_sort():
-            nc.scalar.copy(
+            nc.vector.tensor_copy(
                 out=bc_sorted[:].rearrange("p t (m e) -> p t m e", e=4),
                 in_=bc_rows[:].rearrange("p (m t e) -> p t m e", t=4, e=4),
             )
@@ -156,7 +162,7 @@ def tile_analogue_rain_downscaling_s9_kernel(tc, x, w_words, w_scales, b, corr, 
 
         def r_weave(g, fh, part, on_vector):
             if (g, fh) not in r_il:
-                r_il[g, fh] = keep.tile([P, 4 * N], BF16, name="r_il%d%d" % (g, fh), tag="r_il", bufs=5, align_bytes=64)
+                r_il[g, fh] = keep.tile([P, 4 * N], BF16, name="r_il%d%d" % (g, fh), tag="r_il", bufs=6, align_bytes=64)
             lo, hi = ((0, 256), (256, N), (0, N))[part]
             dst = r_il[g, fh][:, 4 * lo : 4 * hi].rearrange("p (c i t) -> p c t i", i=4, t=4)
             src = r_raw[g][:, :, N * fh + lo : N * fh + hi].rearrange("p t (c i) -> p c t i", i=4)
@@ -223,8 +229,9 @@ def tile_analogue_rain_downscaling_s9_kernel(tc, x, w_words, w_scales, b, corr, 
         pair = {}
 
         def pair_add(hf, g):
-            pair[hf, g] = keep.tile([P, 2, 3 * P], F32, name="pair%d%d" % (hf, g), tag="h_il%d" % ((g - 1) % 4), align_bytes=64)
-            nc.gpsimd.tensor_tensor(out=pair[hf, g][:], in0=kern[hf, g][:, 0:2, 0 : 3 * P], in1=kern[hf, g][:, 2:4, 0 : 3 * P], op=ALU.add)
+            w = PAIRED[hf] * P
+            pair[hf, g] = keep.tile([P, 2, w], F32, name="pair%d%d" % (hf, g), tag="h_il%d" % ((g - 1) % 4), align_bytes=64)
+            nc.gpsimd.tensor_tensor(out=pair[hf, g][:], in0=kern[hf, g][:, 0:2, 0:w], in1=kern[hf, g][:, 2:4, 0:w], op=ALU.add)
 
         def mean_turn(hf, blocks, bk, first, last):
             if first:
@@ -240,8 +247,11 @@ def tile_analogue_rain_downscaling_s9_kernel(tc, x, w_words, w_scales, b, corr, 
                 )
 
         def step_blocks(hf, g):
-            blocks = [(3, kern[hf, g][:, t, 3 * P :]) for t in range(4)]
-            return blocks + [(j, pair[hf, g][:, u, P * j : P * (j + 1)]) for u in range(2) for j in range(3)]
+            blocks = [(j, kern[hf, g][:, t, P * j : P * (j + 1)]) for t in range(4) for j in range(PAIRED[hf], 4)]
+            return blocks + [(j, pair[hf, g][:, u, P * j : P * (j + 1)]) for u in range(2) for j in range(PAIRED[hf])]
+
+        def whole_blocks(hf, g):
+            return [(j, kern[hf, g][:, t, P * j : P * (j + 1)]) for t in range(4) for j in range(4)]
 
         def kern_rows(hf, g):
             return [kern[hf, g][:, t, :] for t in range(4)]
@@ -256,6 +266,12 @@ def tile_analogue_rain_downscaling_s9_kernel(tc, x, w_words, w_scales, b, corr, 
         def mean_sum(hf):
             total[hf] = keep.tile([P, 4], F32, name="total%d" % hf)
             nc.vector.tensor_reduce(out=total[hf][:], in_=m_ps[hf][:], axis=mybir.AxisListType.X, op=ALU.add)
+
+        def mean_on_scalar(hf):
+            mean[hf] = keep.tile([P, 4], F32, name="mean%d" % hf)
+            spill = keep.tile([P, 4, P], F32, name="spill%d" % hf, tag="spill")
+            for j in range(4):
+                nc.scalar.activation(out=spill[:, j, :], in_=m_ps[hf][:, j, :], func=ACT.Copy, scale=1.0 / A, accum_out=mean[hf][:, j : j + 1])
 
         def mean_scale(hf):
             mean[hf] = keep.tile([P, 4], F32, name="mean%d" % hf)
@@ -303,39 +319,40 @@ def tile_analogue_rain_downscaling_s9_kernel(tc, x, w_words, w_scales, b, corr, 
 
         V, S = True, False
         warm(WARM)
+        bc_sort()
         x_turn(0, 0, 0, 4)
+        bc_turn_pe(3)
         x_turn(0, 0, 1, 5)
         x_out(0, 0, 0, S)
         x_out(0, 0, 1, V)
+        bc_out()
         x_turn(0, 1, 0, 6)
         x_turn(0, 1, 1, 7)
-        bc_sort()
-        bc_turn_pe(3)
-        warm(3)
-        x_quant(0, 0)
-        s_sort(0)
+        warm(2)
+        x_turn(1, 0, 0, 4)
+        x_turn(1, 0, 1, 5)
         x_out(0, 1, 0, S)
-        x_out(0, 1, 1, V)
-        bc_out()
+        x_quant(0, 0)
+        x_out(0, 1, 1, S)
+        s_sort(0)
+        x_quant(0, 1, 0, 256)
         w_sort(0)
-        x_quant(0, 1)
+        x_quant(0, 1, 256, N)
+        x_out(1, 0, 0, S)
+        x_out(1, 0, 1, S)
 
         scores(0, 0)
         w_sort(1)
         for g in range(1, 4):
             s_sort(g)
-        r_weave(0, 0, 2, V)
+        x_quant(1, 0)
         w_sort(2)
         w_sort(3)
         pair_add(0, 0)
         h_make(0, 0)
 
         scores(0, 1)
-        x_turn(1, 0, 0, 5)
-        x_turn(1, 0, 1, 6)
-        x_out(1, 0, 0, S)
-        x_out(1, 0, 1, S)
-        r_weave(0, 1, 2, V)
+        r_weave(0, 0, 2, V)
         h_quant(0, 0)
         pair_add(0, 1)
         h_make(0, 1)
@@ -345,8 +362,6 @@ def tile_analogue_rain_downscaling_s9_kernel(tc, x, w_words, w_scales, b, corr, 
         x_turn(1, 1, 1, 6)
         x_out(1, 1, 0, S)
         x_out(1, 1, 1, S)
-        x_quant(1, 0)
-        r_quant(0, 0)
         x_quant(1, 1)
         h_quant(0, 1)
         pair_add(0, 2)
@@ -354,63 +369,67 @@ def tile_analogue_rain_downscaling_s9_kernel(tc, x, w_words, w_scales, b, corr, 
 
         scores(0, 3)
         mean_turn(0, step_blocks(0, 0), 4, True, False)
-        r_weave(1, 0, 0, S)
-        r_quant(0, 1)
-        r_weave(2, 0, 2, V)
+        r_weave(0, 1, 0, S)
+        r_weave(1, 0, 2, V)
         h_quant(0, 2)
         pair_add(0, 3)
         h_make(0, 3)
 
         scores(1, 0)
         mean_turn(0, step_blocks(0, 1), 4, False, False)
-        r_weave(1, 0, 1, S)
-        r_quant(2, 0)
-        r_weave(1, 1, 2, V)
+        r_weave(3, 0, 0, S)
+        r_quant(0, 0)
+        r_weave(2, 0, 2, V)
         r_quant(1, 0)
+        r_weave(0, 1, 1, V)
+        r_quant(2, 0)
 
         scores(1, 1)
         mean_turn(0, step_blocks(0, 2), 4, False, False)
-        r_weave(3, 0, 0, S)
+        r_weave(3, 0, 1, S)
+        r_quant(3, 0)
         h_quant(0, 3)
         pair_add(1, 0)
         h_make(1, 0)
 
         scores(1, 2)
         mean_turn(0, step_blocks(0, 3), 4, False, True)
-        r_weave(3, 0, 1, S)
         mean_sum(0)
-        r_quant(3, 0)
+        r_quant(0, 1)
         mean_scale(0)
-        r_quant(1, 1)
+        r_weave(1, 1, 2, V)
         mean_invert(0)
-        r_weave(2, 1, 2, V)
 
         scores(1, 3)
-        r_weave(3, 1, 2, S)
+        r_weave(2, 1, 2, S)
+        r_weave(3, 1, 0, S)
+        r_weave(3, 1, 1, V)
+        r_quant(1, 1)
+        r_quant(2, 1)
+        r_quant(3, 1)
         h_quant(1, 0)
         pair_add(1, 1)
         h_make(1, 1)
-        r_quant(2, 1)
-        r_quant(3, 1)
+        for j in range(4):
+            y_group(0, j, 0, (5, 6, 0, 1)[j], S)
+        mean_turn(1, step_blocks(1, 0) + whole_blocks(1, 3), 4, True, False)
         h_quant(1, 1)
         pair_add(1, 2)
         h_make(1, 2)
-        for j in range(4):
-            y_group(0, j, 0, (5, 6, 0, 1)[j], S)
-        mean_turn(1, step_blocks(1, 0) + step_blocks(1, 1), 4, True, False)
         h_quant(1, 2)
-        pair_add(1, 3)
         h_make(1, 3)
         for j in range(4):
             y_group(0, j, 1, (2, 7, 5, 6)[j], S)
-        h_quant(1, 3)
-        for g in range(3):
-            y_pass(1, 0, 0, g, 0)
-        mean_turn(1, step_blocks(1, 2) + step_blocks(1, 3), 4, False, True)
+        mean_turn(1, step_blocks(1, 1) + step_blocks(1, 2), 4, False, True)
         mean_sum(1)
+        h_quant(1, 3)
         mean_scale(1)
         mean_invert(1)
-        y_pass(1, 0, 0, 3, 0)
-        y_out(1, 0, 0, S)
-        for i in range(1, 8):
-            y_group(1, i // 2, i % 2, (0, 1, 2, 7, 5, 6, 3, 4)[i], i % 2 == 1, 2 if i == 7 else 1)
+        banks = (0, 1, 2, 7, 5, 6, 3, 4)
+        for g in range(4):
+            for i in range(EARLY):
+                y_pass(1, i // 2, i % 2, g, banks[i])
+        for i in range(EARLY):
+            y_out(1, i // 2, i % 2, i % 2 == 1)
+        for i in range(EARLY, 8):
+            y_group(1, i // 2, i % 2, banks[i], i % 2 == 1, 2 if i == 7 else 1)

@@ -19,226 +19,233 @@ ALU = mybir.AluOpType
 
 P = 128
 N = 512
-WARM = 3
-PAIRED = (3, 3)
+SLOTS = 4
+TILES = N // P
+GROUPS = A // N
+HALF_N = N // 2
+
+SCORE_BANKS = (0, 1, 2, 7)
+GAIN_BANK = 3
+MEAN_BANK = 4
+TURN_BANKS = (5, 6)
+
+PAIRED = 3
 EARLY = 5
+WARM_FIRST, WARM_SECOND = 4, 2
 
 
 def tile_analogue_rain_downscaling_s9_kernel(tc, x, w_words, w_scales, b, corr, rain, out):
     nc = tc.nc
     with ExitStack() as ctx:
-        keep = ctx.enter_context(tc.tile_pool(name="keep", bufs=1))
+        sbuf = ctx.enter_context(tc.tile_pool(name="sbuf", bufs=1))
         psum = ctx.enter_context(tc.psum_pool(name="psum", bufs=1))
         ctx.enter_context(tc.manual_schedule())
+
+        def sb_tile(shape, dtype, name, tag=None, bufs=1):
+            return sbuf.tile(shape, dtype, name=name, tag=tag or name, bufs=bufs, align_bytes=64)
 
         def bank(i, shape, name):
             return psum.tile(shape, F32, name=name, tag="bank%d" % i)
 
-        s_raw = [keep.tile([P, 2, P], I32, name="s_raw0", align_bytes=64), keep.tile([P, 2, 3 * P], I32, name="s_raw1", align_bytes=64)]
-        bc_rows = keep.tile([P, N], BF16, name="bc_rows", align_bytes=64)
-        zeros = keep.tile([P, N], BF16, name="zeros", align_bytes=64)
-        ident = keep.tile([P, P], F32, name="ident", align_bytes=64)
-        nc.vector.memset(bc_rows[:], 0.0)
+        def move(on_vector, dst, src):
+            if on_vector:
+                nc.vector.tensor_copy(out=dst, in_=src)
+            else:
+                nc.scalar.copy(out=dst, in_=src)
+
+        def quantise(src, fmt, codes, scales):
+            nc.vector.quantize_mx(out=codes.bitcast(fmt), scales=scales, in_=src)
+
+        ws_raw = [sb_tile([P, 2, 2 * P], I32, "ws_raw%d" % i) for i in range(2)]
+        bc_rows = sb_tile([2 * GROUPS, N], BF16, "bc_rows")
+        zeros = sb_tile([P, N], BF16, "zeros")
+        ident = sb_tile([P, P], F32, "ident")
+        bc_sorted = sb_tile([P, SLOTS, P], F32, "bc_sorted")
+        nc.vector.memset(ws_raw[0][:], 0)
         nc.vector.memset(zeros[:], 0.0)
-        nc.vector.memset(s_raw[0][:], 0)
-        nc.vector.memset(s_raw[1][:], 0)
+        nc.vector.memset(ws_raw[1][:], 0)
+        nc.vector.memset(bc_sorted[:], 0.0)
         make_identity(nc, ident[:])
-        table = keep.tile([P, 1], F32, name="table")
+
+        exp_warm = sb_tile([P, 1], F32, "exp_warm")
+        nc.scalar.activation(out=exp_warm[:], in_=zeros[:, 0:1], func=ACT.Exp)
+
+        def warm_tensor(count):
+            scratch = bank(SCORE_BANKS[0], [P, N], "scratch")
+            for i in range(count):
+                nc.tensor.matmul(out=scratch[:], lhsT=zeros[:, 0:P], rhs=zeros[:], start=True, stop=True)
 
         x_raw, w_raw, r_raw = {}, {}, {}
 
         def load_x(hf, k, j0, j1):
-            raw = keep.tile([P, j1 - j0, N], BF16, name="x_raw%d%d%d" % (hf, k, j0), align_bytes=64)
+            raw = sb_tile([P, j1 - j0, N], BF16, "x_raw%d%d%d" % (hf, k, j0))
             src = x[N * hf + P * j0 : N * hf + P * j1, N * k : N * (k + 1)].rearrange("(j p) c -> p j c", p=P)
             nc.sync.dma_start(out=raw[:], in_=src)
             for j in range(j0, j1):
                 x_raw[hf, k, j] = raw[:, j - j0, :]
 
-        def load_w(g0, g1):
-            raw = keep.tile([P, 2, 256 * (g1 - g0)], I32, name="w_raw%d" % g0, align_bytes=64)
-            src = w_words.bitcast(I32).rearrange("k p n -> p k n")[:, :, 256 * g0 : 256 * g1]
+        def load_w(g0, g1, tag):
+            raw = sb_tile([P, 2, HALF_N * (g1 - g0)], I32, "w_raw%d" % g0, tag)
+            src = w_words.bitcast(I32).rearrange("k p n -> p k n")[:, :, HALF_N * g0 : HALF_N * g1]
             nc.sync.dma_start(out=raw[:], in_=src)
             for g in range(g0, g1):
-                w_raw[g] = raw[:, :, 256 * (g - g0) : 256 * (g - g0 + 1)]
+                w_raw[g] = raw[:, :, HALF_N * (g - g0) : HALF_N * (g - g0 + 1)]
 
-        def load_scales(i):
-            lo, hi = ((0, P), (P, 4 * P))[i]
-            src = w_scales.bitcast(I32).rearrange("k q n -> q k n")
+        def load_w_scales(i):
+            src = w_scales.bitcast(I32).rearrange("k row n -> row k n")[:, :, 2 * P * i : 2 * P * (i + 1)]
             for q in range(4):
-                nc.sync.dma_start(out=s_raw[i][32 * q : 32 * q + 4, :, :], in_=src[4 * q : 4 * q + 4, :, lo:hi])
+                nc.sync.dma_start(out=ws_raw[i][32 * q : 32 * q + 4, :, :], in_=src[4 * q : 4 * q + 4])
 
         def load_rain(g):
-            r_raw[g] = keep.tile([P, 4, F], BF16, name="r_raw%d" % g, align_bytes=64)
-            src = rain[N * g : N * (g + 1), :].rearrange("(m t e) f -> e m t f", t=4, e=4)
+            r_raw[g] = sb_tile([P, SLOTS, F], BF16, "r_raw%d" % g)
+            src = rain[N * g : N * (g + 1), :].rearrange("(m t e) f -> e m t f", t=SLOTS, e=4)
             for e in range(4):
                 nc.sync.dma_start(out=r_raw[g][e:P:4, :, :], in_=src[e])
 
-        nc.scalar.dma_start(out=bc_rows[0:4, :], in_=b.rearrange("(g a) -> g a", g=4))
-        nc.scalar.dma_start(out=bc_rows[4:8, :], in_=corr.rearrange("(g a) -> g a", g=4))
-        nc.scalar.activation(out=table[:], in_=zeros[:, 0:1], func=ACT.Exp)
-        for k in range(2):
-            load_x(0, k, 0, 2)
-            load_x(0, k, 2, 4)
-        load_w(0, 1)
-        load_scales(0)
-        load_x(1, 0, 0, 4)
-        load_w(1, 2)
-        load_scales(1)
-        load_w(2, 4)
-        load_rain(0)
-        load_x(1, 1, 0, 4)
-        load_rain(1)
-        load_rain(2)
-        load_rain(3)
+        def h_tag(g):
+            return "h_place%d" % (g % GROUPS)
 
-        def warm(n):
-            scratch = bank(0, [P, N], "scratch")
-            for i in range(n):
-                nc.tensor.matmul(out=scratch[:], lhsT=zeros[:, 0:P], rhs=zeros[:], start=True, stop=True)
+        nc.sync.dma_start(out=bc_rows[0:GROUPS, :], in_=b.rearrange("(g a) -> g a", g=GROUPS))
+        nc.sync.dma_start(out=bc_rows[GROUPS:, :], in_=corr.rearrange("(g a) -> g a", g=GROUPS))
+        load_x(0, 0, 0, TILES)
+        load_x(0, 1, 0, TILES // 2)
+        load_x(0, 1, TILES // 2, TILES)
+        load_w(0, 1, "w_raw0")
+        load_w_scales(0)
+        load_w(1, 2, "w_raw1")
+        load_rain(0)
+        load_w_scales(1)
+        load_w(2, GROUPS, h_tag(-1))
+        load_x(1, 0, 0, TILES)
+        load_x(1, 1, 0, TILES)
+        for g in range(1, GROUPS):
+            load_rain(g)
+
+        bias = sb_tile([P, GROUPS, SLOTS], F32, "bias")
+        bc_ps = bank(GAIN_BANK, [P, SLOTS, P], "bc_ps")
+
+        def turn_b_and_corr():
+            nc.vector.tensor_copy(
+                out=bc_sorted[0 : 2 * GROUPS].rearrange("p t (m e) -> p t m e", e=4),
+                in_=bc_rows[:].rearrange("p (m t e) -> p t m e", t=SLOTS, e=4),
+            )
+            for t in range(SLOTS):
+                nc.tensor.transpose(bc_ps[:, t, :], bc_sorted[:, t, :], ident[:])
+            nc.scalar.copy(out=bias[:], in_=bc_ps[:, :, 0:GROUPS].rearrange("p t g -> p g t"))
 
         x_ps, x_il, x_q, x_s = {}, {}, {}, {}
 
         def x_turn(hf, k, jj, bk):
-            ps = bank(bk, [P, 2, 2, P], "x_ps%d%d%d" % (hf, k, jj))
-            x_ps[hf, k, jj] = ps
+            x_ps[hf, k, jj] = bank(bk, [P, 2, 2, P], "x_ps%d%d%d" % (hf, k, jj))
             for j in range(2):
                 words = x_raw[hf, k, 2 * jj + j].bitcast(F32)
                 for u in range(2):
-                    nc.tensor.transpose(ps[:, j, u, :], words[:, u:256:2], ident[:])
+                    nc.tensor.transpose(x_ps[hf, k, jj][:, j, u, :], words[:, u:HALF_N:2], ident[:])
 
         def x_out(hf, k, jj, on_vector):
-            if (hf, k) not in x_il:
-                x_il[hf, k] = keep.tile([P, 4 * N], BF16, name="x_il%d%d" % (hf, k), tag="x_il", bufs=3, align_bytes=64)
-            dst = x_il[hf, k][:, 1024 * jj : 1024 * (jj + 1)].bitcast(F32).rearrange("p (j r u) -> p j r u", j=2, u=2)
-            src = x_ps[hf, k, jj][:].rearrange("p j u r -> p j r u")
-            if on_vector:
-                nc.vector.tensor_copy(out=dst, in_=src)
-            else:
-                nc.scalar.copy(out=dst, in_=src)
+            if jj == 0:
+                x_il[hf, k] = sb_tile([P, SLOTS * N], BF16, "x_il%d%d" % (hf, k), "x_il", 3)
+            dst = x_il[hf, k][:, 2 * N * jj : 2 * N * (jj + 1)].bitcast(F32).rearrange("p (j r u) -> p j r u", j=2, u=2)
+            move(on_vector, dst, x_ps[hf, k, jj][:].rearrange("p j u r -> p j r u"))
 
         def x_quant(hf, k, c0=0, c1=N):
             if c0 == 0:
-                x_q[hf, k] = keep.tile([P, N], U32, name="x_q%d%d" % (hf, k), align_bytes=64)
-                x_s[hf, k] = keep.tile([P, N], U8, name="x_s%d%d" % (hf, k), align_bytes=64)
-            nc.vector.quantize_mx(out=x_q[hf, k][:, c0:c1].bitcast(E4M3), scales=x_s[hf, k][:, c0:c1], in_=x_il[hf, k][:, 4 * c0 : 4 * c1])
+                x_q[hf, k] = sb_tile([P, N], U32, "x_q%d%d" % (hf, k))
+                x_s[hf, k] = sb_tile([P, N], U8, "x_s%d%d" % (hf, k))
+            quantise(x_il[hf, k][:, SLOTS * c0 : SLOTS * c1], E4M3, x_q[hf, k][:, c0:c1], x_s[hf, k][:, c0:c1])
 
         w_q, w_s = {}, {}
 
         def w_sort(g):
-            w_q[g] = keep.tile([P, 2 * 1024], U8, name="w_q%d" % g, align_bytes=64)
+            w_q[g] = sb_tile([P, 2 * 2 * N], U8, "w_q%d" % g)
             nc.vector.tensor_copy(
-                out=w_q[g][:].bitcast(I32).rearrange("p (k t m i) -> p k t m i", k=2, t=4, i=2),
-                in_=w_raw[g].rearrange("p k (m t i) -> p k t m i", t=4, i=2),
+                out=w_q[g][:].bitcast(I32).rearrange("p (k t m i) -> p k t m i", k=2, t=SLOTS, i=2),
+                in_=w_raw[g].rearrange("p k (m t i) -> p k t m i", t=SLOTS, i=2),
             )
 
-        def s_sort(g):
-            w_s[g] = keep.tile([P, 2 * N], U8, name="w_s%d" % g, align_bytes=64)
+        def w_scale_sort(g):
+            w_s[g] = sb_tile([P, 2 * N], U8, "w_s%d" % g)
             nc.vector.tensor_copy(
-                out=w_s[g][:].bitcast(I32).rearrange("p (k t m) -> p k t m", k=2, t=4),
-                in_=(s_raw[0][:] if g == 0 else s_raw[1][:, :, P * (g - 1) : P * g]).rearrange("p k (m t) -> p k t m", t=4),
+                out=w_s[g][:].bitcast(I32).rearrange("p (k t m) -> p k t m", k=2, t=SLOTS),
+                in_=ws_raw[g // 2][:, :, P * (g % 2) : P * (g % 2 + 1)].rearrange("p k (m t) -> p k t m", t=SLOTS),
             )
-
-        bc_sorted = keep.tile([P, 4, P], F32, name="bc_sorted", align_bytes=64)
-        bias = keep.tile([P, 4, 4], F32, name="bias", align_bytes=64)
-
-        def bc_sort():
-            nc.vector.tensor_copy(
-                out=bc_sorted[:].rearrange("p t (m e) -> p t m e", e=4),
-                in_=bc_rows[:].rearrange("p (m t e) -> p t m e", t=4, e=4),
-            )
-
-        bc_ps = {}
-
-        def bc_turn_pe(bk):
-            bc_ps[0] = bank(bk, [P, 4, P], "bc_ps")
-            for t in range(4):
-                nc.tensor.transpose(bc_ps[0][:, t, :], bc_sorted[:, t, :], ident[:])
-
-        def bc_out():
-            ps = bc_ps[0]
-            nc.scalar.copy(out=bias[:], in_=ps[:, :, 0:4].rearrange("p t g -> p g t"))
 
         r_il, r_q, r_s = {}, {}, {}
 
-        def r_weave(g, fh, part, on_vector):
-            if (g, fh) not in r_il:
-                r_il[g, fh] = keep.tile([P, 4 * N], BF16, name="r_il%d%d" % (g, fh), tag="r_il", bufs=6, align_bytes=64)
-            lo, hi = ((0, 256), (256, N), (0, N))[part]
-            dst = r_il[g, fh][:, 4 * lo : 4 * hi].rearrange("p (c i t) -> p c t i", i=4, t=4)
-            src = r_raw[g][:, :, N * fh + lo : N * fh + hi].rearrange("p t (c i) -> p c t i", i=4)
-            if on_vector:
-                nc.vector.tensor_copy(out=dst, in_=src)
-            else:
-                nc.scalar.copy(out=dst, in_=src)
+        def r_weave(g, fh, on_vector, c0=0, c1=N):
+            if c0 == 0:
+                r_il[g, fh] = sb_tile([P, SLOTS * N], BF16, "r_il%d%d" % (g, fh), "r_il", 6)
+            dst = r_il[g, fh][:, SLOTS * c0 : SLOTS * c1].rearrange("p (c i t) -> p c t i", i=4, t=SLOTS)
+            move(on_vector, dst, r_raw[g][:, :, N * fh + c0 : N * fh + c1].rearrange("p t (c i) -> p c t i", i=4))
 
         def r_quant(g, fh):
-            r_q[g, fh] = keep.tile([P, N], U32, name="r_q%d%d" % (g, fh), align_bytes=64)
-            r_s[g, fh] = keep.tile([P, N], U8, name="r_s%d%d" % (g, fh), align_bytes=64)
-            nc.vector.quantize_mx(out=r_q[g, fh][:].bitcast(E4M3), scales=r_s[g, fh][:], in_=r_il[g, fh][:])
+            r_q[g, fh] = sb_tile([P, N], U32, "r_q%d%d" % (g, fh))
+            r_s[g, fh] = sb_tile([P, N], U8, "r_s%d%d" % (g, fh))
+            quantise(r_il[g, fh][:], E4M3, r_q[g, fh][:], r_s[g, fh][:])
 
-        kern, h_il, h_q, h_s = {}, {}, {}, {}
+        score_ps, kern, h_il, h_q, h_s = {}, {}, {}, {}, {}
 
-        def score(hf, g, t, bk):
+        def score_pass(hf, g, t, k):
+            if k == 0:
+                score_ps[t] = bank(SCORE_BANKS[t], [P, N], "score%d%d%d" % (hf, g, t))
+            col = N * k + P * t
+            nc.tensor.matmul_mx(
+                out=score_ps[t][:],
+                lhsT=w_q[g][:, 2 * col : 2 * (col + P)].bitcast(E2M1),
+                lhsT_scale=w_s[g][:, col : col + P],
+                rhs=x_q[hf, k][:].bitcast(E4M3),
+                rhs_scale=x_s[hf, k][:],
+                start=(k == 0),
+                stop=(k == 1),
+            )
+
+        def score_exp(hf, g, t):
             if t == 0:
-                kern[hf, g] = keep.tile([P, 4, N], F32, name="kern%d%d" % (hf, g), tag="kern", bufs=5, align_bytes=64)
-            ps = bank(bk, [P, N], "sc%d%d%d" % (hf, g, t))
-            for k in range(2):
-                c0 = 1024 * k + 256 * t
-                s0 = N * k + P * t
-                nc.tensor.matmul_mx(
-                    out=ps[:],
-                    lhsT=w_q[g][:, c0 : c0 + 256].bitcast(E2M1),
-                    lhsT_scale=w_s[g][:, s0 : s0 + P],
-                    rhs=x_q[hf, k][:].bitcast(E4M3),
-                    rhs_scale=x_s[hf, k][:],
-                    start=(k == 0),
-                    stop=(k == 1),
-                )
-            nc.scalar.activation(out=kern[hf, g][:, t, :], in_=ps[:], func=ACT.Exp, bias=bias[:, g, t : t + 1])
+                kern[hf, g] = sb_tile([P, SLOTS, N], F32, "kern%d%d" % (hf, g), "kern", GROUPS + 1)
+            nc.scalar.activation(out=kern[hf, g][:, t, :], in_=score_ps[t][:], func=ACT.Exp, bias=bias[:, g, t : t + 1])
+
+        def scores(hf, g):
+            for t in range(SLOTS):
+                score_pass(hf, g, t, 0)
+                score_pass(hf, g, t, 1)
+                score_exp(hf, g, t)
 
         def h_make(hf, g):
-            h_il[hf, g] = keep.tile([P, 4 * N], BF16, name="h_il%d%d" % (hf, g), tag="h_il%d" % g, align_bytes=64)
+            h_il[hf, g] = sb_tile([P, SLOTS * N], BF16, "h_il%d%d" % (hf, g), h_tag(g))
             nc.vector.tensor_tensor(
-                out=h_il[hf, g][:].rearrange("p (c i t) -> p c t i", i=2, t=4),
+                out=h_il[hf, g][:].rearrange("p (c i t) -> p c t i", i=2, t=SLOTS),
                 in0=kern[hf, g][:].rearrange("p t (c i) -> p c t i", i=2),
-                in1=bc_ps[0][:, :, 4 + g : 5 + g].unsqueeze(1).to_broadcast([P, N // 2, 4, 2]),
+                in1=bc_ps[:, :, GROUPS + g : GROUPS + g + 1].unsqueeze(1).to_broadcast([P, HALF_N, SLOTS, 2]),
                 op=ALU.mult,
             )
 
         def h_quant(hf, g):
-            h_q[hf, g] = keep.tile([P, N], U32, name="h_q%d%d" % (hf, g), align_bytes=64)
-            h_s[hf, g] = keep.tile([P, N], U8, name="h_s%d%d" % (hf, g), align_bytes=64)
-            nc.vector.quantize_mx(out=h_q[hf, g][:].bitcast(E5M2), scales=h_s[hf, g][:], in_=h_il[hf, g][:])
+            h_q[hf, g] = sb_tile([P, N], U32, "h_q%d%d" % (hf, g))
+            h_s[hf, g] = sb_tile([P, N], U8, "h_s%d%d" % (hf, g))
+            quantise(h_il[hf, g][:], E5M2, h_q[hf, g][:], h_s[hf, g][:])
 
-        m_ps, inv = {}, {}
-
-        def mean_add(hf, rows, bk, first, last):
-            if first:
-                m_ps[hf] = bank(bk, [P, 4, P], "m_ps%d" % hf)
-            for i, row in enumerate(rows):
-                for j in range(4):
-                    nc.tensor.matmul(
-                        out=m_ps[hf][:, j, :],
-                        lhsT=row[:, P * j : P * (j + 1)],
-                        rhs=ident[:],
-                        is_transpose=True,
-                        start=(first and i == 0 and j == 0),
-                        stop=(last and i == len(rows) - 1 and j == 3),
-                    )
-
-        pair = {}
+        pair, mean_ps, total, mean, inv = {}, {}, {}, {}, {}
 
         def pair_add(hf, g):
-            w = PAIRED[hf] * P
-            pair[hf, g] = keep.tile([P, 2, w], F32, name="pair%d%d" % (hf, g), tag="h_il%d" % ((g - 1) % 4), align_bytes=64)
-            nc.gpsimd.tensor_tensor(out=pair[hf, g][:], in0=kern[hf, g][:, 0:2, 0:w], in1=kern[hf, g][:, 2:4, 0:w], op=ALU.add)
+            width = PAIRED * P
+            pair[hf, g] = sb_tile([P, 2, width], F32, "pair%d%d" % (hf, g), h_tag(g - 1))
+            nc.gpsimd.tensor_tensor(
+                out=pair[hf, g][:], in0=kern[hf, g][:, 0:2, 0:width], in1=kern[hf, g][:, 2:4, 0:width], op=ALU.add
+            )
 
-        def mean_turn(hf, blocks, bk, first, last):
+        def kern_blocks(hf, g, j0):
+            return [(j, kern[hf, g][:, t, P * j : P * (j + 1)]) for t in range(SLOTS) for j in range(j0, TILES)]
+
+        def paired_blocks(hf, g):
+            sums = [(j, pair[hf, g][:, u, P * j : P * (j + 1)]) for u in range(2) for j in range(PAIRED)]
+            return kern_blocks(hf, g, PAIRED) + sums
+
+        def mean_turn(hf, blocks, first=False, last=False):
             if first:
-                m_ps[hf] = bank(bk, [P, 4, P], "m_ps%d" % hf)
+                mean_ps[hf] = bank(MEAN_BANK, [P, TILES, P], "mean_ps%d" % hf)
             for i, (j, block) in enumerate(blocks):
                 nc.tensor.matmul(
-                    out=m_ps[hf][:, j, :],
+                    out=mean_ps[hf][:, j, :],
                     lhsT=block,
                     rhs=ident[:],
                     is_transpose=True,
@@ -246,39 +253,16 @@ def tile_analogue_rain_downscaling_s9_kernel(tc, x, w_words, w_scales, b, corr, 
                     stop=(last and i == len(blocks) - 1),
                 )
 
-        def step_blocks(hf, g):
-            blocks = [(j, kern[hf, g][:, t, P * j : P * (j + 1)]) for t in range(4) for j in range(PAIRED[hf], 4)]
-            return blocks + [(j, pair[hf, g][:, u, P * j : P * (j + 1)]) for u in range(2) for j in range(PAIRED[hf])]
-
-        def whole_blocks(hf, g):
-            return [(j, kern[hf, g][:, t, P * j : P * (j + 1)]) for t in range(4) for j in range(4)]
-
-        def kern_rows(hf, g):
-            return [kern[hf, g][:, t, :] for t in range(4)]
-
-        def add(name, a, c):
-            res = keep.tile(list(a.shape), F32, name=name, align_bytes=64)
-            nc.vector.tensor_tensor(out=res[:], in0=a, in1=c, op=ALU.add)
-            return res
-
-        total, mean = {}, {}
-
         def mean_sum(hf):
-            total[hf] = keep.tile([P, 4], F32, name="total%d" % hf)
-            nc.vector.tensor_reduce(out=total[hf][:], in_=m_ps[hf][:], axis=mybir.AxisListType.X, op=ALU.add)
-
-        def mean_on_scalar(hf):
-            mean[hf] = keep.tile([P, 4], F32, name="mean%d" % hf)
-            spill = keep.tile([P, 4, P], F32, name="spill%d" % hf, tag="spill")
-            for j in range(4):
-                nc.scalar.activation(out=spill[:, j, :], in_=m_ps[hf][:, j, :], func=ACT.Copy, scale=1.0 / A, accum_out=mean[hf][:, j : j + 1])
+            total[hf] = sb_tile([P, TILES], F32, "total%d" % hf)
+            nc.vector.tensor_reduce(out=total[hf][:], in_=mean_ps[hf][:], axis=mybir.AxisListType.X, op=ALU.add)
 
         def mean_scale(hf):
-            mean[hf] = keep.tile([P, 4], F32, name="mean%d" % hf)
+            mean[hf] = sb_tile([P, TILES], F32, "mean%d" % hf)
             nc.vector.tensor_scalar(out=mean[hf][:], in0=total[hf][:], scalar1=1.0 / A, scalar2=None, op0=ALU.mult)
 
         def mean_invert(hf):
-            inv[hf] = keep.tile([P, 4], F32, name="inv%d" % hf)
+            inv[hf] = sb_tile([P, TILES], F32, "inv%d" % hf)
             nc.vector.reciprocal(out=inv[hf][:], in_=mean[hf][:])
 
         y_ps = {}
@@ -293,143 +277,134 @@ def tile_analogue_rain_downscaling_s9_kernel(tc, x, w_words, w_scales, b, corr, 
                 rhs=r_q[g, fh][:].bitcast(E4M3),
                 rhs_scale=r_s[g, fh][:],
                 start=(g == 0),
-                stop=(g == 3),
+                stop=(g == GROUPS - 1),
             )
 
-        def y_out(hf, j, fh, on_vector, parts=1):
-            res = keep.tile([P, N], F32, name="res%d%d%d" % (hf, j, fh), tag="res", bufs=5, align_bytes=64)
-            r0 = N * hf + P * j
-            w = N // parts
-            for c in range(0, N, w):
-                src = y_ps[hf, j, fh][:, c : c + w]
+        def y_out(hf, j, fh, on_vector, width=N):
+            res = sb_tile([P, N], F32, "res%d%d%d" % (hf, j, fh), "res", EARLY + 1)
+            rows = slice(N * hf + P * j, N * hf + P * (j + 1))
+            factor = inv[hf][:, j : j + 1]
+            for c in range(0, N, width):
+                src, dst = y_ps[hf, j, fh][:, c : c + width], res[:, c : c + width]
                 if on_vector:
-                    nc.vector.tensor_scalar(out=res[:, c : c + w], in0=src, scalar1=inv[hf][:, j : j + 1], scalar2=None, op0=ALU.mult)
+                    nc.vector.tensor_scalar(out=dst, in0=src, scalar1=factor, scalar2=None, op0=ALU.mult)
                 else:
-                    nc.scalar.activation(out=res[:, c : c + w], in_=src, func=ACT.Copy, scale=inv[hf][:, j : j + 1])
-                nc.sync.dma_start(out=out[r0 : r0 + P, N * fh + c : N * fh + c + w], in_=res[:, c : c + w])
+                    nc.scalar.activation(out=dst, in_=src, func=ACT.Copy, scale=factor)
+                nc.sync.dma_start(out=out[rows, N * fh + c : N * fh + c + width], in_=dst)
 
-        def y_group(hf, j, fh, bk, on_vector, parts=1):
-            for g in range(4):
+        def y_group(hf, j, fh, bk, on_vector, width=N):
+            for g in range(GROUPS):
                 y_pass(hf, j, fh, g, bk)
-            y_out(hf, j, fh, on_vector, parts)
+            y_out(hf, j, fh, on_vector, width)
 
-        def scores(hf, g):
-            for t in range(4):
-                score(hf, g, t, (0, 1, 2, 7)[t])
+        def next_h(done, step):
+            h_quant(*done)
+            pair_add(*step)
+            h_make(*step)
 
-        V, S = True, False
-        warm(WARM)
-        bc_sort()
-        x_turn(0, 0, 0, 4)
-        bc_turn_pe(3)
-        x_turn(0, 0, 1, 5)
-        x_out(0, 0, 0, S)
-        x_out(0, 0, 1, V)
-        bc_out()
-        x_turn(0, 1, 0, 6)
-        x_turn(0, 1, 1, 7)
-        warm(2)
-        x_turn(1, 0, 0, 4)
-        x_turn(1, 0, 1, 5)
-        x_out(0, 1, 0, S)
-        x_quant(0, 0)
-        x_out(0, 1, 1, S)
-        s_sort(0)
-        x_quant(0, 1, 0, 256)
+        vector, scalar = True, False
+
+        warm_tensor(WARM_FIRST)
+        turn_b_and_corr()
+        x_turn(0, 0, 0, MEAN_BANK)
+        x_turn(0, 0, 1, TURN_BANKS[0])
+        x_out(0, 0, 0, scalar)
+        x_out(0, 0, 1, vector)
+        x_turn(0, 1, 0, TURN_BANKS[1])
+        x_turn(0, 1, 1, SCORE_BANKS[-1])
+        warm_tensor(WARM_SECOND)
+        x_out(0, 1, 0, scalar)
+        x_out(0, 1, 1, scalar)
         w_sort(0)
-        x_quant(0, 1, 256, N)
-        x_out(1, 0, 0, S)
-        x_out(1, 0, 1, S)
+        x_quant(0, 0)
+        w_scale_sort(0)
+        x_quant(0, 1, 0, HALF_N)
+        x_quant(0, 1, HALF_N, N)
 
-        scores(0, 0)
+        for t0 in range(0, SLOTS, 2):
+            for k in range(2):
+                score_pass(0, 0, t0, k)
+                score_pass(0, 0, t0 + 1, k)
+            score_exp(0, 0, t0)
+            score_exp(0, 0, t0 + 1)
         w_sort(1)
-        for g in range(1, 4):
-            s_sort(g)
-        x_quant(1, 0)
-        w_sort(2)
-        w_sort(3)
+        w_scale_sort(1)
+        r_weave(0, 0, vector)
+        for sort in (w_scale_sort, w_sort):
+            sort(2)
+            sort(3)
         pair_add(0, 0)
         h_make(0, 0)
 
-        scores(0, 1)
-        r_weave(0, 0, 2, V)
-        h_quant(0, 0)
-        pair_add(0, 1)
-        h_make(0, 1)
-
-        scores(0, 2)
-        x_turn(1, 1, 0, 5)
-        x_turn(1, 1, 1, 6)
-        x_out(1, 1, 0, S)
-        x_out(1, 1, 1, S)
-        x_quant(1, 1)
-        h_quant(0, 1)
-        pair_add(0, 2)
-        h_make(0, 2)
+        for k in range(2):
+            scores(0, 1 + k)
+            for jj in range(2):
+                x_turn(1, k, jj, TURN_BANKS[jj])
+            for jj in range(2):
+                x_out(1, k, jj, scalar)
+            if k == 0:
+                r_weave(0, 1, vector)
+            else:
+                x_quant(1, 0)
+                r_quant(0, 0)
+                x_quant(1, 1)
+            next_h((0, k), (0, k + 1))
 
         scores(0, 3)
-        mean_turn(0, step_blocks(0, 0), 4, True, False)
-        r_weave(0, 1, 0, S)
-        r_weave(1, 0, 2, V)
-        h_quant(0, 2)
-        pair_add(0, 3)
-        h_make(0, 3)
+        mean_turn(0, paired_blocks(0, 0), first=True)
+        r_weave(1, 0, vector)
+        next_h((0, 2), (0, 3))
 
         scores(1, 0)
-        mean_turn(0, step_blocks(0, 1), 4, False, False)
-        r_weave(3, 0, 0, S)
-        r_quant(0, 0)
-        r_weave(2, 0, 2, V)
+        mean_turn(0, paired_blocks(0, 1))
+        r_weave(3, 0, scalar, 0, HALF_N)
+        r_quant(0, 1)
+        r_weave(2, 0, vector)
         r_quant(1, 0)
-        r_weave(0, 1, 1, V)
         r_quant(2, 0)
 
         scores(1, 1)
-        mean_turn(0, step_blocks(0, 2), 4, False, False)
-        r_weave(3, 0, 1, S)
+        mean_turn(0, paired_blocks(0, 2))
+        r_weave(3, 0, scalar, HALF_N, N)
         r_quant(3, 0)
-        h_quant(0, 3)
-        pair_add(1, 0)
-        h_make(1, 0)
+        next_h((0, 3), (1, 0))
 
         scores(1, 2)
-        mean_turn(0, step_blocks(0, 3), 4, False, True)
+        mean_turn(0, paired_blocks(0, 3), last=True)
         mean_sum(0)
-        r_quant(0, 1)
+        r_weave(1, 1, vector)
         mean_scale(0)
-        r_weave(1, 1, 2, V)
-        mean_invert(0)
 
         scores(1, 3)
-        r_weave(2, 1, 2, S)
-        r_weave(3, 1, 0, S)
-        r_weave(3, 1, 1, V)
-        r_quant(1, 1)
-        r_quant(2, 1)
-        r_quant(3, 1)
-        h_quant(1, 0)
-        pair_add(1, 1)
-        h_make(1, 1)
-        for j in range(4):
-            y_group(0, j, 0, (5, 6, 0, 1)[j], S)
-        mean_turn(1, step_blocks(1, 0) + whole_blocks(1, 3), 4, True, False)
-        h_quant(1, 1)
-        pair_add(1, 2)
-        h_make(1, 2)
+        r_weave(2, 1, scalar)
+        r_weave(3, 1, scalar, 0, HALF_N)
+        r_weave(3, 1, vector, HALF_N, N)
+        mean_invert(0)
+        for g in range(1, GROUPS):
+            r_quant(g, 1)
+
+        free_banks = TURN_BANKS + SCORE_BANKS
+        next_h((1, 0), (1, 1))
+        for j in range(TILES):
+            y_group(0, j, 0, free_banks[j], scalar)
+        mean_turn(1, paired_blocks(1, 0) + kern_blocks(1, 3, 0), first=True)
+        next_h((1, 1), (1, 2))
         h_quant(1, 2)
         h_make(1, 3)
-        for j in range(4):
-            y_group(0, j, 1, (2, 7, 5, 6)[j], S)
-        mean_turn(1, step_blocks(1, 1) + step_blocks(1, 2), 4, False, True)
+        for j in range(TILES):
+            y_group(0, j, 1, free_banks[(TILES + j) % len(free_banks)], scalar)
+        mean_turn(1, paired_blocks(1, 1) + paired_blocks(1, 2), last=True)
         mean_sum(1)
         h_quant(1, 3)
         mean_scale(1)
         mean_invert(1)
-        banks = (0, 1, 2, 7, 5, 6, 3, 4)
-        for g in range(4):
+
+        groups = [(j, fh) for j in range(TILES) for fh in range(2)]
+        last_banks = SCORE_BANKS + TURN_BANKS + (GAIN_BANK, MEAN_BANK)
+        for g in range(GROUPS):
             for i in range(EARLY):
-                y_pass(1, i // 2, i % 2, g, banks[i])
+                y_pass(1, *groups[i], g, last_banks[i])
         for i in range(EARLY):
-            y_out(1, i // 2, i % 2, i % 2 == 1)
-        for i in range(EARLY, 8):
-            y_group(1, i // 2, i % 2, banks[i], i % 2 == 1, 2 if i == 7 else 1)
+            y_out(1, *groups[i], i % 2 == 1)
+        for i in range(EARLY, len(groups)):
+            y_group(1, *groups[i], last_banks[i], i % 2 == 1, HALF_N if i == len(groups) - 1 else N)

@@ -29,9 +29,8 @@ GAIN_BANK = 3
 MEAN_BANK = 4
 TURN_BANKS = (5, 6)
 
-PAIRED = 3
+PAIRED = (3, 4)
 EARLY = 5
-WARM_FIRST, WARM_SECOND = 4, 2
 
 
 def tile_analogue_rain_downscaling_s9_kernel(tc, x, w_words, w_scales, b, corr, rain, out):
@@ -57,25 +56,19 @@ def tile_analogue_rain_downscaling_s9_kernel(tc, x, w_words, w_scales, b, corr, 
             nc.vector.quantize_mx(out=codes.bitcast(fmt), scales=scales, in_=src)
 
         ws_raw = [sb_tile([P, 2, 2 * P], I32, "ws_raw%d" % i) for i in range(2)]
-        bc_rows = sb_tile([2 * GROUPS, N], BF16, "bc_rows")
-        zeros = sb_tile([P, N], BF16, "zeros")
         ident = sb_tile([P, P], F32, "ident")
-        bc_sorted = sb_tile([P, SLOTS, P], F32, "bc_sorted")
-        nc.vector.memset(ws_raw[0][:], 0)
-        nc.vector.memset(zeros[:], 0.0)
-        nc.vector.memset(ws_raw[1][:], 0)
-        nc.vector.memset(bc_sorted[:], 0.0)
+        corr_sorted = sb_tile([P, SLOTS, P], F32, "corr_sorted")
+        b_sorted = sb_tile([P, SLOTS, P], F32, "b_sorted")
+        for zeroed in (ws_raw[0], corr_sorted, ws_raw[1], b_sorted):
+            nc.vector.memset(zeroed[:], 0)
         make_identity(nc, ident[:])
 
-        exp_warm = sb_tile([P, 1], F32, "exp_warm")
-        nc.scalar.activation(out=exp_warm[:], in_=zeros[:, 0:1], func=ACT.Exp)
-
-        def warm_tensor(count):
-            scratch = bank(SCORE_BANKS[0], [P, N], "scratch")
-            for i in range(count):
-                nc.tensor.matmul(out=scratch[:], lhsT=zeros[:, 0:P], rhs=zeros[:], start=True, stop=True)
-
         x_raw, w_raw, r_raw = {}, {}, {}
+
+        def load_rows(vec, name):
+            rows = sb_tile([GROUPS, N], BF16, name)
+            nc.sync.dma_start(out=rows[:], in_=vec.rearrange("(g a) -> g a", g=GROUPS))
+            return rows
 
         def load_x(hf, k, j0, j1):
             raw = sb_tile([P, j1 - j0, N], BF16, "x_raw%d%d%d" % (hf, k, j0))
@@ -105,8 +98,8 @@ def tile_analogue_rain_downscaling_s9_kernel(tc, x, w_words, w_scales, b, corr, 
         def h_tag(g):
             return "h_place%d" % (g % GROUPS)
 
-        nc.sync.dma_start(out=bc_rows[0:GROUPS, :], in_=b.rearrange("(g a) -> g a", g=GROUPS))
-        nc.sync.dma_start(out=bc_rows[GROUPS:, :], in_=corr.rearrange("(g a) -> g a", g=GROUPS))
+        corr_rows = load_rows(corr, "corr_rows")
+        b_rows = load_rows(b, "b_rows")
         load_x(0, 0, 0, TILES)
         load_x(0, 1, 0, TILES // 2)
         load_x(0, 1, TILES // 2, TILES)
@@ -122,16 +115,22 @@ def tile_analogue_rain_downscaling_s9_kernel(tc, x, w_words, w_scales, b, corr, 
             load_rain(g)
 
         bias = sb_tile([P, GROUPS, SLOTS], F32, "bias")
-        bc_ps = bank(GAIN_BANK, [P, SLOTS, P], "bc_ps")
+        corr_ps = bank(GAIN_BANK, [P, SLOTS, P], "corr_ps")
 
-        def turn_b_and_corr():
+        def sort_rows(dst, rows):
             nc.vector.tensor_copy(
-                out=bc_sorted[0 : 2 * GROUPS].rearrange("p t (m e) -> p t m e", e=4),
-                in_=bc_rows[:].rearrange("p (m t e) -> p t m e", t=SLOTS, e=4),
+                out=dst[0:GROUPS].rearrange("p t (m e) -> p t m e", e=4),
+                in_=rows[:].rearrange("p (m t e) -> p t m e", t=SLOTS, e=4),
             )
+
+        def corr_turn(t):
+            nc.tensor.matmul(out=corr_ps[:, t, :], lhsT=corr_sorted[:, t, :], rhs=ident[:], start=True, stop=True)
+
+        def b_turn(bk):
+            ps = bank(bk, [P, SLOTS, P], "b_ps")
             for t in range(SLOTS):
-                nc.tensor.transpose(bc_ps[:, t, :], bc_sorted[:, t, :], ident[:])
-            nc.scalar.copy(out=bias[:], in_=bc_ps[:, :, 0:GROUPS].rearrange("p t g -> p g t"))
+                nc.tensor.transpose(ps[:, t, :], b_sorted[:, t, :], ident[:])
+            return ps
 
         x_ps, x_il, x_q, x_s = {}, {}, {}, {}
 
@@ -215,7 +214,7 @@ def tile_analogue_rain_downscaling_s9_kernel(tc, x, w_words, w_scales, b, corr, 
             nc.vector.tensor_tensor(
                 out=h_il[hf, g][:].rearrange("p (c i t) -> p c t i", i=2, t=SLOTS),
                 in0=kern[hf, g][:].rearrange("p t (c i) -> p c t i", i=2),
-                in1=bc_ps[:, :, GROUPS + g : GROUPS + g + 1].unsqueeze(1).to_broadcast([P, HALF_N, SLOTS, 2]),
+                in1=corr_ps[:, :, g : g + 1].unsqueeze(1).to_broadcast([P, HALF_N, SLOTS, 2]),
                 op=ALU.mult,
             )
 
@@ -227,20 +226,18 @@ def tile_analogue_rain_downscaling_s9_kernel(tc, x, w_words, w_scales, b, corr, 
         pair, mean_ps, total, mean, inv = {}, {}, {}, {}, {}
 
         def pair_add(hf, g):
-            width = PAIRED * P
+            width = PAIRED[hf] * P
             pair[hf, g] = sb_tile([P, 2, width], F32, "pair%d%d" % (hf, g), h_tag(g - 1))
             nc.gpsimd.tensor_tensor(
                 out=pair[hf, g][:], in0=kern[hf, g][:, 0:2, 0:width], in1=kern[hf, g][:, 2:4, 0:width], op=ALU.add
             )
 
-        def kern_blocks(hf, g, j0):
-            return [(j, kern[hf, g][:, t, P * j : P * (j + 1)]) for t in range(SLOTS) for j in range(j0, TILES)]
+        def mean_blocks(hf, g):
+            single = [(j, kern[hf, g][:, t, P * j : P * (j + 1)]) for t in range(SLOTS) for j in range(PAIRED[hf], TILES)]
+            return single + [(j, pair[hf, g][:, u, P * j : P * (j + 1)]) for u in range(2) for j in range(PAIRED[hf])]
 
-        def paired_blocks(hf, g):
-            sums = [(j, pair[hf, g][:, u, P * j : P * (j + 1)]) for u in range(2) for j in range(PAIRED)]
-            return kern_blocks(hf, g, PAIRED) + sums
-
-        def mean_turn(hf, blocks, first=False, last=False):
+        def mean_turn(hf, g, first=False, last=False):
+            blocks = mean_blocks(hf, g)
             if first:
                 mean_ps[hf] = bank(MEAN_BANK, [P, TILES, P], "mean_ps%d" % hf)
             for i, (j, block) in enumerate(blocks):
@@ -304,17 +301,22 @@ def tile_analogue_rain_downscaling_s9_kernel(tc, x, w_words, w_scales, b, corr, 
 
         vector, scalar = True, False
 
-        warm_tensor(WARM_FIRST)
-        turn_b_and_corr()
+        sort_rows(corr_sorted, corr_rows)
+        sort_rows(b_sorted, b_rows)
+        corr_turn(0)
+        corr_turn(1)
         x_turn(0, 0, 0, MEAN_BANK)
         x_turn(0, 0, 1, TURN_BANKS[0])
         x_out(0, 0, 0, scalar)
         x_out(0, 0, 1, vector)
         x_turn(0, 1, 0, TURN_BANKS[1])
-        x_turn(0, 1, 1, SCORE_BANKS[-1])
-        warm_tensor(WARM_SECOND)
+        x_turn(0, 1, 1, SCORE_BANKS[3])
+        corr_turn(2)
+        corr_turn(3)
+        b_ps = b_turn(SCORE_BANKS[2])
         x_out(0, 1, 0, scalar)
         x_out(0, 1, 1, scalar)
+        nc.scalar.copy(out=bias[:], in_=b_ps[:, :, 0:GROUPS].rearrange("p t g -> p g t"))
         w_sort(0)
         x_quant(0, 0)
         w_scale_sort(0)
@@ -351,12 +353,12 @@ def tile_analogue_rain_downscaling_s9_kernel(tc, x, w_words, w_scales, b, corr, 
             next_h((0, k), (0, k + 1))
 
         scores(0, 3)
-        mean_turn(0, paired_blocks(0, 0), first=True)
+        mean_turn(0, 0, first=True)
         r_weave(1, 0, vector)
         next_h((0, 2), (0, 3))
 
         scores(1, 0)
-        mean_turn(0, paired_blocks(0, 1))
+        mean_turn(0, 1)
         r_weave(3, 0, scalar, 0, HALF_N)
         r_quant(0, 1)
         r_weave(2, 0, vector)
@@ -364,13 +366,13 @@ def tile_analogue_rain_downscaling_s9_kernel(tc, x, w_words, w_scales, b, corr, 
         r_quant(2, 0)
 
         scores(1, 1)
-        mean_turn(0, paired_blocks(0, 2))
+        mean_turn(0, 2)
         r_weave(3, 0, scalar, HALF_N, N)
         r_quant(3, 0)
         next_h((0, 3), (1, 0))
 
         scores(1, 2)
-        mean_turn(0, paired_blocks(0, 3), last=True)
+        mean_turn(0, 3, last=True)
         mean_sum(0)
         r_weave(1, 1, vector)
         mean_scale(0)
@@ -380,20 +382,25 @@ def tile_analogue_rain_downscaling_s9_kernel(tc, x, w_words, w_scales, b, corr, 
         r_weave(3, 1, scalar, 0, HALF_N)
         r_weave(3, 1, vector, HALF_N, N)
         mean_invert(0)
-        for g in range(1, GROUPS):
-            r_quant(g, 1)
+        r_quant(1, 1)
+        pair[1, 3] = sb_tile([P, 2, N], F32, "pair13")
+        nc.vector.tensor_tensor(out=pair[1, 3][:], in0=kern[1, 3][:, 0:2, :], in1=kern[1, 3][:, 2:4, :], op=ALU.add)
+        r_quant(2, 1)
+        r_quant(3, 1)
 
         free_banks = TURN_BANKS + SCORE_BANKS
         next_h((1, 0), (1, 1))
         for j in range(TILES):
             y_group(0, j, 0, free_banks[j], scalar)
-        mean_turn(1, paired_blocks(1, 0) + kern_blocks(1, 3, 0), first=True)
+            if j % 2 == 1:
+                mean_turn(1, 0 if j == 1 else 3, first=(j == 1))
         next_h((1, 1), (1, 2))
         h_quant(1, 2)
         h_make(1, 3)
         for j in range(TILES):
             y_group(0, j, 1, free_banks[(TILES + j) % len(free_banks)], scalar)
-        mean_turn(1, paired_blocks(1, 1) + paired_blocks(1, 2), last=True)
+            if j >= 2:
+                mean_turn(1, j - 1, last=(j == TILES - 1))
         mean_sum(1)
         h_quant(1, 3)
         mean_scale(1)

from contextlib import ExitStack

import concourse.mybir as mybir
from concourse.masks import make_identity

D, C, A, F = 1024, 1024, 2048, 1024
FLOPS = 2 * D * C * A + 2 * D * A * F

F32 = mybir.dt.float32
BF16 = mybir.dt.bfloat16
I32 = mybir.dt.int32
U32 = mybir.dt.uint32
U8 = mybir.dt.uint8
E4M3 = mybir.dt.float8_e4m3fn_x4
E5M2 = mybir.dt.float8_e5m2_x4
E2M1 = mybir.dt.float4_e2m1fn_x4
ACT = mybir.ActivationFunctionType
ALU = mybir.AluOpType

P = 128
N = 512
SLOTS = 4
TILES = N // P
GROUPS = A // N
HALF_N = N // 2

SCORE_BANKS = (0, 1, 2, 7)
GAIN_BANK = 3
MEAN_BANK = 4
TURN_BANKS = (5, 6)

PAIRED = (3, 4)
EARLY = 5


def tile_analogue_rain_downscaling_s9_kernel(tc, x, w_words, w_scales, b, corr, rain, out):
    nc = tc.nc
    with ExitStack() as ctx:
        sbuf = ctx.enter_context(tc.tile_pool(name="sbuf", bufs=1))
        psum = ctx.enter_context(tc.psum_pool(name="psum", bufs=1))
        ctx.enter_context(tc.manual_schedule())

        def sb_tile(shape, dtype, name, tag=None, bufs=1):
            return sbuf.tile(shape, dtype, name=name, tag=tag or name, bufs=bufs, align_bytes=64)

        def bank(i, shape, name):
            return psum.tile(shape, F32, name=name, tag="bank%d" % i)

        def move(on_vector, dst, src):
            if on_vector:
                nc.vector.tensor_copy(out=dst, in_=src)
            else:
                nc.scalar.copy(out=dst, in_=src)

        def quantise(src, fmt, codes, scales):
            nc.vector.quantize_mx(out=codes.bitcast(fmt), scales=scales, in_=src)

        ws_raw = [sb_tile([P, 2, 2 * P], I32, "ws_raw%d" % i) for i in range(2)]
        ident = sb_tile([P, P], F32, "ident")
        corr_sorted = sb_tile([P, SLOTS, P], F32, "corr_sorted")
        b_sorted = sb_tile([P, SLOTS, P], F32, "b_sorted")
        for zeroed in (ws_raw[0], corr_sorted, ws_raw[1], b_sorted):
            nc.vector.memset(zeroed[:], 0)
        make_identity(nc, ident[:])

        x_raw, w_raw, r_raw = {}, {}, {}

        def load_rows(vec, name):
            rows = sb_tile([GROUPS, N], BF16, name)
            nc.sync.dma_start(out=rows[:], in_=vec.rearrange("(g a) -> g a", g=GROUPS))
            return rows

        def load_x(hf, k, j0, j1):
            raw = sb_tile([P, j1 - j0, N], BF16, "x_raw%d%d%d" % (hf, k, j0))
            src = x[N * hf + P * j0 : N * hf + P * j1, N * k : N * (k + 1)].rearrange("(j p) c -> p j c", p=P)
            nc.sync.dma_start(out=raw[:], in_=src)
            for j in range(j0, j1):
                x_raw[hf, k, j] = raw[:, j - j0, :]

        def load_w(g0, g1, tag):
            raw = sb_tile([P, 2, HALF_N * (g1 - g0)], I32, "w_raw%d" % g0, tag)
            src = w_words.bitcast(I32).rearrange("k p n -> p k n")[:, :, HALF_N * g0 : HALF_N * g1]
            nc.sync.dma_start(out=raw[:], in_=src)
            for g in range(g0, g1):
                w_raw[g] = raw[:, :, HALF_N * (g - g0) : HALF_N * (g - g0 + 1)]

        def load_w_scales(i):
            src = w_scales.bitcast(I32).rearrange("k row n -> row k n")[:, :, 2 * P * i : 2 * P * (i + 1)]
            for q in range(4):
                nc.sync.dma_start(out=ws_raw[i][32 * q : 32 * q + 4, :, :], in_=src[4 * q : 4 * q + 4])

        def load_rain(g):
            r_raw[g] = sb_tile([P, SLOTS, F], BF16, "r_raw%d" % g)
            src = rain[N * g : N * (g + 1), :].rearrange("(m t e) f -> e m t f", t=SLOTS, e=4)
            for e in range(4):
                nc.sync.dma_start(out=r_raw[g][e:P:4, :, :], in_=src[e])

        def h_tag(g):
            return "h_place%d" % (g % GROUPS)

        corr_rows = load_rows(corr, "corr_rows")
        b_rows = load_rows(b, "b_rows")
        load_x(0, 0, 0, TILES)
        load_x(0, 1, 0, TILES // 2)
        load_x(0, 1, TILES // 2, TILES)
        load_w(0, 1, "w_raw0")
        load_w_scales(0)
        load_w(1, 2, "w_raw1")
        load_rain(0)
        load_w_scales(1)
        load_w(2, GROUPS, h_tag(-1))
        load_x(1, 0, 0, TILES)
        load_x(1, 1, 0, TILES)
        for g in range(1, GROUPS):
            load_rain(g)

        bias = sb_tile([P, GROUPS, SLOTS], F32, "bias")
        corr_ps = bank(GAIN_BANK, [P, SLOTS, P], "corr_ps")

        def sort_rows(dst, rows):
            nc.vector.tensor_copy(
                out=dst[0:GROUPS].rearrange("p t (m e) -> p t m e", e=4),
                in_=rows[:].rearrange("p (m t e) -> p t m e", t=SLOTS, e=4),
            )

        def corr_turn(t):
            nc.tensor.matmul(out=corr_ps[:, t, :], lhsT=corr_sorted[:, t, :], rhs=ident[:], start=True, stop=True)

        def b_turn(bk):
            ps = bank(bk, [P, SLOTS, P], "b_ps")
            for t in range(SLOTS):
                nc.tensor.transpose(ps[:, t, :], b_sorted[:, t, :], ident[:])
            return ps

        x_ps, x_il, x_q, x_s = {}, {}, {}, {}

        def x_turn(hf, k, jj, bk):
            x_ps[hf, k, jj] = bank(bk, [P, 2, 2, P], "x_ps%d%d%d" % (hf, k, jj))
            for j in range(2):
                words = x_raw[hf, k, 2 * jj + j].bitcast(F32)
                for u in range(2):
                    nc.tensor.transpose(x_ps[hf, k, jj][:, j, u, :], words[:, u:HALF_N:2], ident[:])

        def x_out(hf, k, jj, on_vector):
            if jj == 0:
                x_il[hf, k] = sb_tile([P, SLOTS * N], BF16, "x_il%d%d" % (hf, k), "x_il", 3)
            dst = x_il[hf, k][:, 2 * N * jj : 2 * N * (jj + 1)].bitcast(F32).rearrange("p (j r u) -> p j r u", j=2, u=2)
            move(on_vector, dst, x_ps[hf, k, jj][:].rearrange("p j u r -> p j r u"))

        def x_quant(hf, k, c0=0, c1=N):
            if c0 == 0:
                x_q[hf, k] = sb_tile([P, N], U32, "x_q%d%d" % (hf, k))
                x_s[hf, k] = sb_tile([P, N], U8, "x_s%d%d" % (hf, k))
            quantise(x_il[hf, k][:, SLOTS * c0 : SLOTS * c1], E4M3, x_q[hf, k][:, c0:c1], x_s[hf, k][:, c0:c1])

        w_q, w_s = {}, {}

        def w_sort(g):
            w_q[g] = sb_tile([P, 2 * 2 * N], U8, "w_q%d" % g)
            nc.vector.tensor_copy(
                out=w_q[g][:].bitcast(I32).rearrange("p (k t m i) -> p k t m i", k=2, t=SLOTS, i=2),
                in_=w_raw[g].rearrange("p k (m t i) -> p k t m i", t=SLOTS, i=2),
            )

        def w_scale_sort(g):
            w_s[g] = sb_tile([P, 2 * N], U8, "w_s%d" % g)
            nc.vector.tensor_copy(
                out=w_s[g][:].bitcast(I32).rearrange("p (k t m) -> p k t m", k=2, t=SLOTS),
                in_=ws_raw[g // 2][:, :, P * (g % 2) : P * (g % 2 + 1)].rearrange("p k (m t) -> p k t m", t=SLOTS),
            )

        r_il, r_q, r_s = {}, {}, {}

        def r_weave(g, fh, on_vector, c0=0, c1=N):
            if c0 == 0:
                r_il[g, fh] = sb_tile([P, SLOTS * N], BF16, "r_il%d%d" % (g, fh), "r_il", 6)
            dst = r_il[g, fh][:, SLOTS * c0 : SLOTS * c1].rearrange("p (c i t) -> p c t i", i=4, t=SLOTS)
            move(on_vector, dst, r_raw[g][:, :, N * fh + c0 : N * fh + c1].rearrange("p t (c i) -> p c t i", i=4))

        def r_quant(g, fh):
            r_q[g, fh] = sb_tile([P, N], U32, "r_q%d%d" % (g, fh))
            r_s[g, fh] = sb_tile([P, N], U8, "r_s%d%d" % (g, fh))
            quantise(r_il[g, fh][:], E4M3, r_q[g, fh][:], r_s[g, fh][:])

        score_ps, kern, h_il, h_q, h_s = {}, {}, {}, {}, {}

        def score_pass(hf, g, t, k):
            if k == 0:
                score_ps[t] = bank(SCORE_BANKS[t], [P, N], "score%d%d%d" % (hf, g, t))
            col = N * k + P * t
            nc.tensor.matmul_mx(
                out=score_ps[t][:],
                lhsT=w_q[g][:, 2 * col : 2 * (col + P)].bitcast(E2M1),
                lhsT_scale=w_s[g][:, col : col + P],
                rhs=x_q[hf, k][:].bitcast(E4M3),
                rhs_scale=x_s[hf, k][:],
                start=(k == 0),
                stop=(k == 1),
            )

        def score_exp(hf, g, t):
            if t == 0:
                kern[hf, g] = sb_tile([P, SLOTS, N], F32, "kern%d%d" % (hf, g), "kern", GROUPS + 1)
            nc.scalar.activation(out=kern[hf, g][:, t, :], in_=score_ps[t][:], func=ACT.Exp, bias=bias[:, g, t : t + 1])

        def scores(hf, g):
            for t in range(SLOTS):
                score_pass(hf, g, t, 0)
                score_pass(hf, g, t, 1)
                score_exp(hf, g, t)

        def h_make(hf, g):
            h_il[hf, g] = sb_tile([P, SLOTS * N], BF16, "h_il%d%d" % (hf, g), h_tag(g))
            nc.vector.tensor_tensor(
                out=h_il[hf, g][:].rearrange("p (c i t) -> p c t i", i=2, t=SLOTS),
                in0=kern[hf, g][:].rearrange("p t (c i) -> p c t i", i=2),
                in1=corr_ps[:, :, g : g + 1].unsqueeze(1).to_broadcast([P, HALF_N, SLOTS, 2]),
                op=ALU.mult,
            )

        def h_quant(hf, g):
            h_q[hf, g] = sb_tile([P, N], U32, "h_q%d%d" % (hf, g))
            h_s[hf, g] = sb_tile([P, N], U8, "h_s%d%d" % (hf, g))
            quantise(h_il[hf, g][:], E5M2, h_q[hf, g][:], h_s[hf, g][:])

        pair, mean_ps, total, mean, inv = {}, {}, {}, {}, {}

        def pair_add(hf, g):
            width = PAIRED[hf] * P
            pair[hf, g] = sb_tile([P, 2, width], F32, "pair%d%d" % (hf, g), h_tag(g - 1))
            nc.gpsimd.tensor_tensor(
                out=pair[hf, g][:], in0=kern[hf, g][:, 0:2, 0:width], in1=kern[hf, g][:, 2:4, 0:width], op=ALU.add
            )

        def mean_blocks(hf, g):
            single = [(j, kern[hf, g][:, t, P * j : P * (j + 1)]) for t in range(SLOTS) for j in range(PAIRED[hf], TILES)]
            return single + [(j, pair[hf, g][:, u, P * j : P * (j + 1)]) for u in range(2) for j in range(PAIRED[hf])]

        def mean_turn(hf, g, first=False, last=False):
            blocks = mean_blocks(hf, g)
            if first:
                mean_ps[hf] = bank(MEAN_BANK, [P, TILES, P], "mean_ps%d" % hf)
            for i, (j, block) in enumerate(blocks):
                nc.tensor.matmul(
                    out=mean_ps[hf][:, j, :],
                    lhsT=block,
                    rhs=ident[:],
                    is_transpose=True,
                    start=(first and i == 0),
                    stop=(last and i == len(blocks) - 1),
                )

        def mean_sum(hf):
            total[hf] = sb_tile([P, TILES], F32, "total%d" % hf)
            nc.vector.tensor_reduce(out=total[hf][:], in_=mean_ps[hf][:], axis=mybir.AxisListType.X, op=ALU.add)

        def mean_scale(hf):
            mean[hf] = sb_tile([P, TILES], F32, "mean%d" % hf)
            nc.vector.tensor_scalar(out=mean[hf][:], in0=total[hf][:], scalar1=1.0 / A, scalar2=None, op0=ALU.mult)

        def mean_invert(hf):
            inv[hf] = sb_tile([P, TILES], F32, "inv%d" % hf)
            nc.vector.reciprocal(out=inv[hf][:], in_=mean[hf][:])

        y_ps = {}

        def y_pass(hf, j, fh, g, bk):
            if g == 0:
                y_ps[hf, j, fh] = bank(bk, [P, N], "y%d%d%d" % (hf, j, fh))
            nc.tensor.matmul_mx(
                out=y_ps[hf, j, fh][:],
                lhsT=h_q[hf, g][:, P * j : P * (j + 1)].bitcast(E5M2),
                lhsT_scale=h_s[hf, g][:, P * j : P * (j + 1)],
                rhs=r_q[g, fh][:].bitcast(E4M3),
                rhs_scale=r_s[g, fh][:],
                start=(g == 0),
                stop=(g == GROUPS - 1),
            )

        def y_out(hf, j, fh, on_vector, width=N):
            res = sb_tile([P, N], F32, "res%d%d%d" % (hf, j, fh), "res", EARLY + 1)
            rows = slice(N * hf + P * j, N * hf + P * (j + 1))
            factor = inv[hf][:, j : j + 1]
            for c in range(0, N, width):
                src, dst = y_ps[hf, j, fh][:, c : c + width], res[:, c : c + width]
                if on_vector:
                    nc.vector.tensor_scalar(out=dst, in0=src, scalar1=factor, scalar2=None, op0=ALU.mult)
                else:
                    nc.scalar.activation(out=dst, in_=src, func=ACT.Copy, scale=factor)
                nc.sync.dma_start(out=out[rows, N * fh + c : N * fh + c + width], in_=dst)

        def y_group(hf, j, fh, bk, on_vector, width=N):
            for g in range(GROUPS):
                y_pass(hf, j, fh, g, bk)
            y_out(hf, j, fh, on_vector, width)

        def next_h(done, step):
            h_quant(*done)
            pair_add(*step)
            h_make(*step)

        vector, scalar = True, False

        sort_rows(corr_sorted, corr_rows)
        sort_rows(b_sorted, b_rows)
        corr_turn(0)
        corr_turn(1)
        x_turn(0, 0, 0, MEAN_BANK)
        x_turn(0, 0, 1, TURN_BANKS[0])
        x_out(0, 0, 0, scalar)
        x_out(0, 0, 1, vector)
        x_turn(0, 1, 0, TURN_BANKS[1])
        x_turn(0, 1, 1, SCORE_BANKS[3])
        corr_turn(2)
        corr_turn(3)
        b_ps = b_turn(SCORE_BANKS[2])
        x_out(0, 1, 0, scalar)
        x_out(0, 1, 1, scalar)
        nc.scalar.copy(out=bias[:], in_=b_ps[:, :, 0:GROUPS].rearrange("p t g -> p g t"))
        w_sort(0)
        x_quant(0, 0)
        w_scale_sort(0)
        x_quant(0, 1, 0, HALF_N)
        x_quant(0, 1, HALF_N, N)

        for t0 in range(0, SLOTS, 2):
            for k in range(2):
                score_pass(0, 0, t0, k)
                score_pass(0, 0, t0 + 1, k)
            score_exp(0, 0, t0)
            score_exp(0, 0, t0 + 1)
        w_sort(1)
        w_scale_sort(1)
        r_weave(0, 0, vector)
        for sort in (w_scale_sort, w_sort):
            sort(2)
            sort(3)
        pair_add(0, 0)
        h_make(0, 0)

        for k in range(2):
            scores(0, 1 + k)
            for jj in range(2):
                x_turn(1, k, jj, TURN_BANKS[jj])
            for jj in range(2):
                x_out(1, k, jj, scalar)
            if k == 0:
                r_weave(0, 1, vector)
            else:
                x_quant(1, 0)
                r_quant(0, 0)
                x_quant(1, 1)
            next_h((0, k), (0, k + 1))

        scores(0, 3)
        mean_turn(0, 0, first=True)
        r_weave(1, 0, vector)
        next_h((0, 2), (0, 3))

        scores(1, 0)
        mean_turn(0, 1)
        r_weave(3, 0, scalar, 0, HALF_N)
        r_quant(0, 1)
        r_weave(2, 0, vector)
        r_quant(1, 0)
        r_quant(2, 0)

        scores(1, 1)
        mean_turn(0, 2)
        r_weave(3, 0, scalar, HALF_N, N)
        r_quant(3, 0)
        next_h((0, 3), (1, 0))

        scores(1, 2)
        mean_turn(0, 3, last=True)
        mean_sum(0)
        r_weave(1, 1, vector)
        mean_scale(0)

        scores(1, 3)
        r_weave(2, 1, scalar)
        r_weave(3, 1, scalar, 0, HALF_N)
        r_weave(3, 1, vector, HALF_N, N)
        mean_invert(0)
        r_quant(1, 1)
        pair[1, 3] = sb_tile([P, 2, N], F32, "pair13")
        nc.vector.tensor_tensor(out=pair[1, 3][:], in0=kern[1, 3][:, 0:2, :], in1=kern[1, 3][:, 2:4, :], op=ALU.add)
        r_quant(2, 1)
        r_quant(3, 1)

        free_banks = TURN_BANKS + SCORE_BANKS
        next_h((1, 0), (1, 1))
        for j in range(TILES):
            y_group(0, j, 0, free_banks[j], scalar)
            if j % 2 == 1:
                mean_turn(1, 0 if j == 1 else 3, first=(j == 1))
        next_h((1, 1), (1, 2))
        h_quant(1, 2)
        h_make(1, 3)
        for j in range(TILES):
            y_group(0, j, 1, free_banks[(TILES + j) % len(free_banks)], scalar)
            if j >= 2:
                mean_turn(1, j - 1, last=(j == TILES - 1))
        mean_sum(1)
        h_quant(1, 3)
        mean_scale(1)
        mean_invert(1)

        groups = [(j, fh) for j in range(TILES) for fh in range(2)]
        last_banks = SCORE_BANKS + TURN_BANKS + (GAIN_BANK, MEAN_BANK)
        for g in range(GROUPS):
            for i in range(EARLY):
                y_pass(1, *groups[i], g, last_banks[i])
        for i in range(EARLY):
            y_out(1, *groups[i], i % 2 == 1)
        for i in range(EARLY, len(groups)):
            y_group(1, *groups[i], last_banks[i], i % 2 == 1, HALF_N if i == len(groups) - 1 else N)
